import numpy as np, ml_dtypes
CORES = [10,34,74,98]
N = 4
BF = ml_dtypes.bfloat16
def gentries(a):
    return np.ascontiguousarray(a.reshape(8, 16, -1).transpose(0, 2, 1)).reshape(8, -1)
def gtable(e):
    e = np.asarray(e); return np.ascontiguousarray(e.reshape(8, -1, 16).transpose(0, 2, 1)).reshape(128, -1).astype(np.int32)
E, T, C, RO = 4096, 256, 4, 4
A = N * T
VM = 0.125
def floats(rng, far):
    def size(n):
        if far: return np.exp2(-rng.integers(0, 3, (N, 8, 1, n))).astype(np.float32)
        return 0.75 + 0.25 * rng.random((N, 8, 1, n), dtype=np.float32)
    x = 0.25 + 0.75 * rng.random((N, 8, 16, T), dtype=np.float32)
    if far: x = x * size(T)
    u = 0.1875 * (0.5 + 0.5 * rng.random((N, 8, 16, E), dtype=np.float32)) * size(E)
    v = VM * (0.5 + 0.5 * rng.random((N, 8, 16, E), dtype=np.float32)) * size(E)
    w = np.exp(1.5 * rng.standard_normal((N, 128, 128))); w = w * np.reciprocal(np.add.reduce(w, axis=1, keepdims=True))
    one = np.arange(128)[None, :, None] == np.argsort(rng.random((N, 128)), axis=1)[:, None, :]
    share = 0.5 + 0.45 * rng.random((N, 1, 128))
    return x, u, v, (1.3 + 0.08 * rng.random((N, 1, 128))) * (share * one + (1.0 - share) * w)
def lone(rng, fl, b):
    x, u, v, m = fl; a = int(rng.integers(0, N)); c = (a + 1) % N
    u[:, b] = 0.1875 * (0.9375 + 0.0625 * rng.random((N, 16, E)))
    v[:, b] = VM * (0.875 + 0.125 * rng.random((N, 16, E)))
    level = np.where(np.argsort(rng.random(T)) < 3 * T // 8, 0.18 + 0.07 * rng.random(T), 0.0625 + 0.0125 * rng.random(T))
    x[a, b] = np.maximum(level[None, :] * (0.9375 + 0.125 * rng.random((16, T))), 0.0625)
    i = 16 * b + np.arange(16); m[a] = 0.0625 * m[a]; m[a][:, i] = 0.0
    m[a][np.ix_(i, i)] = 1.38 * (0.9 * np.eye(16) + 0.1 * 0.0625)
    p = np.argsort(rng.random(128))[:16]; w = 0.5 + 0.5 * rng.random((128, 16))
    m[c][:, p] = 1.38 * w * np.reciprocal(np.add.reduce(w, axis=0, keepdims=True))
    return x, u, v, m
def small(rng):
    q = rng.integers(-4, 5, (N, 8, 16, T), dtype=np.int32); q[:, :, 15] = rng.integers(-8, 33, (N, 8, T))
    k = rng.integers(-4, 5, (N, 8, 16, E), dtype=np.int32); k[:, :, 15] = rng.integers(-2, 3, (N, 8, E))
    return q, k, rng.integers(0, E, (N, 8, C, A), dtype=np.int32)
def pack(fl, q, k, n):
    x, u, v, m = fl
    return {"x0": x.reshape(N, 128, T).astype(BF), "rq": q.reshape(N, 128, T).astype(np.float32).astype(BF), "ke": k.reshape(N, 128, E).astype(np.float32).astype(BF),
            "ue": u.reshape(N, 128, E).astype(BF), "ve": v.reshape(N, 128, E).astype(BF), "nm": np.stack([gtable(a.reshape(8, -1)) for a in n]), "mm": m.astype(np.float32).astype(BF)}
def route(q, k, n):
    k = k.astype(np.int32); n = n.astype(np.int32)
    qa = np.ascontiguousarray(q.astype(np.int32).transpose(1, 2, 0, 3)).reshape(8, 16, A)
    h = np.zeros((8, A), np.int32); wins = []; names = []
    for l in range(RO):
        nn = (n + h[None, :, None, :]) & (E - 1); w = np.zeros((N, 8, A), np.int32)
        for s in range(N):
            c = np.take_along_axis(k[s], nn[s].reshape(8, 1, C * A), 2).reshape(8, 16, C, A)
            score = np.add.reduce(c * qa[:, :, None, :], axis=1)
            best = np.argmax(score, axis=1)
            w[s] = np.take_along_axis(nn[s], best[:, None, :], 1)[:, 0]
            count = np.bincount((w[s] + E * np.arange(8)[:, None]).reshape(-1), minlength=8 * E).reshape(8, E)
            k[s, :, 15] += np.sign(1 - count).astype(np.int32)
        h = np.roll(np.add.reduce(w, axis=0) & (E - 1), 1, axis=0).astype(np.int32)
        wins.append(w); names.append(nn)
    return wins, names, k[:, :, 15]
def setup_inputs(rng):
    return pack(floats(rng, False), *small(rng))
def setup_inputs_spread(rng):
    q = np.rint(np.exp2(5 * rng.random((N, 8, 1, T))) * (2 * rng.random((N, 8, 16, T)) - 1)).astype(np.int32)
    q[:, :, 15] = np.rint(np.exp2(5 * rng.random((N, 8, T))))
    k = np.rint(np.exp2(5 * rng.random((N, 8, 1, E))) * (2 * rng.random((N, 8, 16, E)) - 1)).astype(np.int32)
    k[:, :, 15] = np.where(rng.random((N, 8, E)) < 0.5, rng.integers(-2, 3, (N, 8, E)), rng.integers(-32, 33, (N, 8, E)))
    n = np.minimum((E * rng.random((N, 8, C, A)) ** 3).astype(np.int32), E - 1)
    return pack(floats(rng, True), q, k, n)
def setup_inputs_ends(rng):
    q = (64 * rng.integers(0, 2, (N, 8, 16, T)) - 32).astype(np.int32); a = rng.random((N, 8, 1, T))
    q = np.where(a < 0.35, 32, np.where(a < 0.5, -32, q)); q[..., T - 1] = 32; q[..., 0] = -32
    k = (64 * rng.integers(0, 2, (N, 8, 16, E)) - 32).astype(np.int32); a = rng.random((N, 8, 1, E))
    k = np.where(a < 0.3, 32, np.where(a < 0.4, -32, k))
    kind = rng.integers(0, 3, (N, 8)); kind[N - 1, 7] = 0; kind[0, 0] = 1; kind[0, 1] = 2
    k[..., E - 1] = np.where((kind < 2)[:, :, None], 32, k[..., E - 1]); k[..., 0] = np.where((kind == 0)[:, :, None], 32, np.where((kind == 1)[:, :, None], -32, k[..., 0]))
    n = (E - 1) * rng.integers(0, 2, (N, 8, C, A))
    n[:, 8 - RO:7, :, A - 1] = E - 1; n[:, 7, :, A - 1] = (E - 1) * (np.arange(C) % 2)
    wins, names, b = route(q, k, n)
    for s in range(N):
        for g in range(8):
            used = np.zeros(E, bool); last = np.zeros(E, bool)
            for l in range(RO - 1): used[names[l][s, g].reshape(-1)] = True
            last[names[RO - 1][s, g].reshape(-1)] = True
            e = np.nonzero(last & ~used)[0]
            k[s, g][:, e] = np.where(rng.random(e.size) < 0.7, 32, -32)
            if g == 7:
                e = names[RO - 1][s, g, :, A - 1]; k[s, g][:, e[~used[e]]] = 32
    return pack(floats(rng, False), q, k, n)
def setup_inputs_crowd(rng):
    q, k, n = small(rng); q[:, :6, 15] = rng.integers(1, 33, (N, 6, T)); k[:, :6, :15] = rng.integers(-4, 5, (N, 6, 15, 1))
    o = rng.permutation(A); n[:, :2] = rng.integers(0, E, (N, 2, C, 1))
    for s in range(N):
        for g in range(2, 8):
            p = rng.permutation(E); v = n[s, g]
            if g < 4:
                v[:] = p[:C, None]; v[:, o[0]] = p[C:2 * C]
            elif g < 6:
                v[:, o[:256]] = p[:C, None]; v[:, o[256:511]] = p[C:2 * C, None]; v[:, o[511:]] = p[rng.integers(2 * C, E, (C, A - 511))]
            else:
                v[:] = p[rng.integers(0, 4, (C, A))]
    return pack(floats(rng, False), q, k, n)
def setup_inputs_calm(rng):
    q, k, n = small(rng); q[:, :, 0] = rng.integers(8, 17, (N, 8, T))
    a = rng.integers(1, 33, (N, 8, T)); q[:, :, 15] = np.where(rng.random((N, 8, T)) < 0.125, -a, a)
    tp = np.argsort(rng.random((8, A)), axis=1)[:, :16]
    for g in range(8): q[tp[g] // T, g, :, tp[g] % T] = np.array([1, 1] + [32] * 13 + [1])
    for s in range(0, N, 2):
        for g in range(8):
            size = np.argsort(rng.random((A // 4, 4)), axis=1).reshape(-1) + 1
            fam = np.repeat(np.arange(size.size), size)[:A]; F = int(fam[-1]) + 1
            p = rng.permutation(E); ex = p[:F * C].reshape(F, C); pair = p[E - 16:].reshape(2, 8)
            n[s, g] = ex[fam[rng.permutation(A)]].T
            k[s, g][:, ex] = rng.integers(-4, 5, (16, F, 1))
            k[s, g, 15][ex] = np.clip(rng.choice(np.array([0, 0, 0, -32, 32]), (F, 1)) + rng.integers(-2, 3, (F, C)), -32, 32)
            lead = rng.random(F) < 0.25; d = rng.integers(0, C, F)
            k[s, g, 0][ex[lead]] = np.where(np.arange(C)[None, :] == d[lead][:, None], 32, -32)
            k[s, g][:, pair[0]] = np.array([32, 31] + [32] * 13 + [-32])[:, None]
            k[s, g][:, pair[1]] = np.array([1 - RO, 1 - RO] + [32] * 13 + [32])[:, None]
            n[s, g][:, tp[g]] = np.where(np.arange(C)[:, None] % 2 == 0, np.repeat(pair[0], 2)[None, :], np.repeat(pair[1], 2)[None, :])
        k[s + 1] = k[s][:, :, (-np.arange(E)) % E]; n[s + 1] = (-n[s]) % E
    return pack(floats(rng, False), q, k, n)
def setup_inputs_corners(rng):
    q, k, n = small(rng)
    q[:, 0] *= (rng.random((N, 1, T)) < 0.5)
    n[:, 1] = n[:, 1, :1]; n[:, 2, C // 2:] = n[:, 2, :C // 2].copy()
    n[:, 3] = rng.choice(np.array([0, 1, E // 2, E - 1]), (N, C, A))
    k[:, 4, :15] = 0; q[:, 4, 15] = rng.choice(np.array([0, 1, -1, 32, -32]), (N, T))
    k[:, 5, :15] = k[:, 5, :15, :1].copy(); q[:, 5, 15] *= (rng.random((N, T)) < 0.75)
    q[:, 6] = rng.integers(-32, 33, (N, 16, T)); k[:, 6] = rng.integers(-32, 33, (N, 16, E))
    k[:, 7] = k[:, 7][:, :, np.arange(E) // 2 * 2]
    k[:, :, 15, 0] = 32; k[:, :, 15, E - 1] = -32
    return pack(lone(rng, floats(rng, False), 6), q, k, n)
def check_ranges(d):
    bad = []
    for a, lo, hi in (("rq", -32, 32), ("ke", -32, 32), ("nm", 0, E - 1)):
        v = np.asarray(d[a]).astype(np.float64)
        if not bool(np.all((v >= lo) & (v <= hi))): bad.append("range of " + a)
        elif not bool(np.all(np.floor(v) == v)): bad.append("whole numbers of " + a)
    for a, lo, hi in (("x0", 0.0625, 1.0), ("ue", 0.0234375, 0.1875), ("ve", 0.125 * VM, VM), ("mm", 0.0, 1.4)):
        v = np.asarray(d[a]).astype(np.float64)
        if not bool(np.all((v >= lo) & (v <= hi))): bad.append("range of " + a)
    if not bool(np.all(np.add.reduce(np.asarray(d["mm"]).astype(np.float64), axis=1) <= 1.4)): bad.append("column sums of mm")
    return bad
def reference(x0, rq, ke, ue, ve, nm, mm):
    q = rq.astype(np.float32).astype(np.int32).reshape(N, 8, 16, T); k = ke.astype(np.float32).astype(np.int32).reshape(N, 8, 16, E)
    n = np.stack([gentries(a) for a in nm]).reshape(N, 8, C, A)
    wins, names, b = route(q, k, n)
    x = np.ascontiguousarray(x0.astype(np.float64).reshape(N, 8, 16, T).transpose(1, 2, 0, 3)).reshape(8, 16, A)
    u = ue.astype(np.float64).reshape(N, 8, 16, E); v = ve.astype(np.float64).reshape(N, 8, 16, E); m = mm.astype(np.float64)
    for l in range(RO):
        y = np.zeros((8, 16, A))
        for s in range(N):
            w = wins[l][s][:, None, :]
            d = np.add.reduce(np.take_along_axis(u[s], w, 2) * x, axis=1)
            y = y + (0.5 * d * (1.0 + np.tanh(0.5 * d)))[:, None, :] * np.take_along_axis(v[s], w, 2)
        z = (0.5 * x + 0.25 * y).reshape(128, N, T)
        x = np.stack([np.tanh(m[r].T @ z[:, r]) for r in range(N)], axis=1).reshape(8, 16, A)
    return {"yx": np.ascontiguousarray(x.reshape(128, N, T).transpose(1, 0, 2)).astype(np.float32), "yb": b.astype(np.float32)}

def check_inputs(d):
    bad = list(check_ranges(d))
    if not bad:
        for name, y in reference(**d).items():
            for q in range(N):
                v = np.abs(np.asarray(y[q], np.float64)); s = np.sqrt(np.mean(v * v))
                if v.max() > 7 * s or s < 2.0 ** -5: bad.append('%s of rank %d is uneven or too small' % (name, q))
    return bad

@@ -1,0 +1,525 @@
+from concourse.bass import DstId, RemoteDMATransfer
+from concourse.mybir import AluOpType, ActivationFunctionType
+
+N, E, TK, C, RO = 4, 4096, 256, 4, 4
+REP = 16
+RUNS = ([(v, 4) for v in range(0, 16, 4)] + [(v, 8) for v in range(16, 64, 8)], [(v, 16) for v in range(0, 64, 16)])
+OC = (0, 6, 8)
+CH = (0, 4, 6, 8)
+F32, BF, I32, U16, F16 = "float32", "bfloat16", "int32", "uint16", "float16"
+
+SCRATCH = {
+    "K": ("sbuf", [128, E], BF), "Uw": ("sbuf", [128, E], BF), "Vw": ("sbuf", [128, E], BF),
+    "nmI": ("sbuf", [128, 256], I32), "nmC": ("sbuf", [128, 256], F32), "qa": ("sbuf", [128, 1024], BF),
+    "off": ("sbuf", [128, 256], U16), "woff": ("sbuf", [128, 64], U16),
+    "prod": ("sbuf", [128, 4096], F16), "kraw": ("sbuf", [128, 3072], BF),
+    "tI": ("sbuf", [128, 256], I32), "tA": ("sbuf", [128, 256], I32),
+    "Xh": ("sbuf", [128, 128], F32), "eyeF": ("sbuf", [128, 128], F32), "X2": ("sbuf", [128, 512], F32),
+    "run": ("sbuf", [128, 256], F32), "old": ("sbuf", [128, 256], F32), "win": ("sbuf", [128, 256], F32),
+    "rst": ("sbuf", [128, 256], F32), "ci": ("sbuf", [128, 8, 8], I32), "DI": ("sbuf", [128, 16, 8], I32),
+    "DR": ("sbuf", [128, REP, 16, 8], BF), "X": ("sbuf", [128, 16, 16], BF), "OH": ("sbuf", [128, 64, 16, 8], BF),
+    "bias": ("sbuf", [128, 256], BF), "biasF": ("sbuf", [128, 256], F32),
+    "Wl": ("sbuf", [128, 3 * 256], F32), "UVs": ("sbuf", [128, RO * N * 512], BF), "UVl": ("sbuf", [128, RO * N * 512], BF),
+    "xB": ("sbuf", [128, 256], BF), "xS": ("sbuf", [128, 256], F32), "xo": ("sbuf", [128, 256], F32),
+    "mmB": ("sbuf", [128, 128], BF), "mmF": ("sbuf", [128, 144], F32),
+    "Pf": ("sbuf", [128, 1024], F32), "Yf": ("sbuf", [128, 1024], F32), "tt": ("sbuf", [128, 256], F32), "sS": ("sbuf", [128, 256], F32),
+    "pI": ("sbuf", [128, 2], I32), "cI": ("sbuf", [128, 8], I32), "cF": ("sbuf", [128, 8], F32), "cG": ("sbuf", [128, 8], F32),
+    "Jn": ("sbuf", [128, 128], F32), "Jd": ("sbuf", [128, 64], F32), "Jb": ("sbuf", [128, 128], F32),
+    "rS": ("sbuf", [128, 8], F16), "rC": ("sbuf", [128, 64], F32), "rL": ("sbuf", [128, 128], BF), "eye": ("sbuf", [128, 128], BF),
+    "quart": ("sbuf", [128, 128], F32), "t4": ("sbuf", [128, 1024], F32), "one": ("sbuf", [128, 4], F32),
+    "dsel": ("sbuf", [128, 256], F32), "bsel": ("sbuf", [128, 512], F32),
+}
+for _b in range(8):
+    SCRATCH["P%d" % _b] = ("psum", [128, 512], F32)
+SEMAPHORES = (["cV", "cA", "cP", "cG", "ldq", "ldn", "ldk", "ldb", "ldx", "lduv", "bias0", "bias1", "bias2", "outb", "outx", "sent", "arrq"]
+              + ["arrW%d" % l for l in range(RO - 1)] + ["arrU%d_%d" % (l, k) for l in range(RO) for k in range(N - 1)])
+
+
+def rank_program(g, core, T, topo):
+    rank = T.rank_of(core)
+    if rank is None:
+        return
+    A, AF = AluOpType, ActivationFunctionType
+    Q = {"V": g.vector, "A": g.scalar, "P": g.tensor, "G": g, "S": g.sync}
+    total, seen, lastw, readers, bank = {}, {k: {} for k in Q}, {}, {}, {}
+
+    def need(q, ev):
+        s, v = ev[0], ev[1]
+        if seen[q].get(s, 0) < v:
+            Q[q].wait_ge(T.sem[s], v)
+            seen[q][s] = v
+
+    def order(q, r, w, b, dma):
+        evs = []
+        for x in r:
+            evs += [e for e in lastw.get(x, []) if dma or e[2] != q or q != "P"]
+        for x in w:
+            evs += [e for e in lastw.get(x, []) + readers.get(x, []) if dma or e[2] != q]
+        for x in b:
+            evs += [e for e in bank.get(x, {}).values() if e[2] != q]
+        top = {}
+        for e in evs:
+            top[e[0]] = max(top.get(e[0], 0), e[1])
+        for s in top:
+            need(q, (s, top[s]))
+
+    def note(ev, r, w, b):
+        for x in r:
+            readers.setdefault(x, []).append(ev)
+        for x in w:
+            lastw[x] = [ev]
+            readers[x] = []
+        for x in b:
+            bank.setdefault(x, {})[ev[2]] = ev
+
+    def op(q, fn, r=(), w=(), b=()):
+        order(q, r, w, b, False)
+        s = "c" + q
+        total[s] = total.get(s, 0) + 1
+        fn().then_inc(T.sem[s], 1)
+        note((s, total[s], q), r, w, b)
+
+    def dmas(q, sem, pairs, r=(), w=()):
+        order(q, r, w, (), True)
+        for o, i in pairs:
+            Q[q].dma_start(o, i).then_inc(T.sem[sem], 16)
+        total[sem] = total.get(sem, 0) + 16 * len(pairs)
+        note((sem, total[sem], "dma"), r, w, ())
+
+    def arrives(sem, n, w):
+        total[sem] = total.get(sem, 0) + n
+        lastw[w] = [(sem, total[sem], "far")]
+
+    peers = [(rank + k) % N for k in range(1, N)]
+    eng = [e for e in topo.engines(core, T.cores[peers[0]]) if all(e in topo.engines(core, T.cores[p]) for p in peers)]
+    assert all(topo.may_write(core, T.cores[p]) for p in peers) and len(eng) >= 8
+    eng = eng[:8]
+
+    def bits(es):
+        return sum(1 << e for e in es)
+
+    def dst(p):
+        a = topo.addr(T.cores[p])
+        return DstId(rid=a[0], pnc=a[1])
+
+    def to_all(ap, sem, r):
+        order("G", r, (), (), True)
+        g.remote_dma_fused([RemoteDMATransfer(dst_ids=[dst(p) for p in peers], dma_engine_mask=bits(eng), remote_sem=T.sem[sem],
+                                              srcs=[ap], dsts=[ap] * len(peers))], local_sem=T.sem.sent)
+        total["sent"] = total.get("sent", 0) + len(eng)
+
+    def to_home(l, k, more):
+        p = peers[k]
+        order("G", ["uv%d_%d_0" % (l, p), "uv%d_%d_1" % (l, p)] + more, (), (), True)
+        so, do = (l * N + p) * 512, (l * N + rank) * 512
+        g.remote_dma_fused([RemoteDMATransfer(dst_ids=[dst(p)], dma_engine_mask=bits(eng), remote_sem=T.sem["arrU%d_%d" % (l, k)],
+                                              src=T.UVs[:, so:so + 512], dst=T.UVl[:, do:do + 512])], local_sem=T.sem.sent)
+        total["sent"] = total.get("sent", 0) + len(eng)
+        arrives("arrU%d_%d" % (l, k), len(eng), "far%d_%d" % (l, (rank - k - 1) % N))
+
+    V, S, PE = g.vector, g.scalar, g.tensor
+    SC, CODE = T.P0[:, 0:256], T.P0[:, 256:512]
+    HBS = [("P1", "P2", "P3")] * (RO - 1) + [("P0", "P0", "P0")]
+    KB = ["Kb0", "Kb1", "Kb2"]
+    xP, LP, hP = T.P1[:, 256:512], T.P2[:, 128:192], T.P0[:, 0:64]
+
+    def turned(d, s):
+        return [(d[16:128, :], s[0:112, :]), (d[0:16, :], s[112:128, :])]
+
+    def bias_rows(t, rows, k):
+        out = []
+        for j in range(CH[k] // 2, CH[k + 1] // 2):
+            if j == 0:
+                out += [(t[0:64, 0:64], rows(7, 7)), (t[64:128, 0:64], rows(0, 0))]
+            else:
+                out.append((t[:, 64 * j:64 * j + 64], rows(2 * j - 1, 2 * j)))
+        return out
+
+    own = slice(rank * TK, (rank + 1) * TK)
+    dmas("S", "ldq", [(T.qa[:, own], T.rq[:, :])], w=["qown"])
+    dmas("S", "ldk", [(T.K[:, :], T.ke[:, :])], w=["K"])
+    dmas("A", "ldn", [(T.nmI[:, :], T.nm[:, :])], w=["nmI"])
+    kerows = lambda a, b: T.ke[16 * a + 15:16 * b + 16:16, :]
+    op("G", lambda: g.iota(T.pI[:, :], [[16, 2]], 0, 1), w=["pI"])
+    op("G", lambda: g.iota(T.Jn[:, :], [[1, 128]], 0, 0, allow_small_or_imprecise_dtypes=True), w=["Jn"])
+    op("G", lambda: g.iota(T.Jb[:, :], [[1, 8], [0, 16]], 0, 0, allow_small_or_imprecise_dtypes=True), w=["Jb"])
+    to_all(T.qa[:, own], "arrq", ["qown"])
+    arrives("arrq", 3 * len(eng), "qfar")
+    op("G", lambda: g.iota(T.Jd[:, :], [[0, 2], [1, 32]], 0, 0, allow_small_or_imprecise_dtypes=True), w=["Jd"])
+    SR, AND = A.arith_shift_right, A.bitwise_and
+    p0, p16 = T.pI[:, 0:1], T.pI[:, 1:2]
+    for j, (src, sh, m) in enumerate([(p0, 4, 7), (p0, 0, 31), (p0, 0, 7), (p16, 4, 7), (p0, 3, 1), (p0, 0, 1), (p0, 1, 63), (p0, 0, 127)]):
+        op("V", lambda: V.tensor_scalar(T.cI[:, j:j + 1], src, sh, m, SR, AND), r=["pI"], w=["cI%d" % j])
+    op("V", lambda: V.memset(T.rst[:, :], 0.0), w=["rst0"])
+    op("V", lambda: V.tensor_copy(T.cF[:, :], T.cI[:, :]), r=["cI%d" % j for j in range(8)], w=["cF"])
+    op("V", lambda: V.memset(T.rst[:, 0::4], -100000.0), r=["rst0"], w=["rst"])
+    op("V", lambda: V.memset(T.old[:, 0:1], 0.0), w=["old0"])
+    cf = lambda j: T.cF[:, j:j + 1]
+    cg = lambda j: T.cG[:, j:j + 1]
+    op("V", lambda: V.tensor_scalar(cg(0), cf(3), 8.0, cf(2), A.mult, A.add), r=["cF"], w=["cG0"])
+    op("V", lambda: V.tensor_scalar(T.cG[:, 2:4], T.cF[:, 4:6], 0.0, None, A.is_equal), r=["cF"], w=["cG2"])
+    op("V", lambda: V.tensor_scalar(T.rS[:, :], T.Jn[:, 0:8], cf(3), None, A.is_equal), r=["cF", "Jn"], w=["rS"])
+    op("V", lambda: V.tensor_scalar(T.eye[:, :], T.Jn[:, :], cf(7), None, A.is_equal), r=["cF", "Jn"], w=["eye"])
+    op("V", lambda: V.tensor_scalar(cg(1), cg(0), 131072.0, None, A.mult), r=["cG0"], w=["cG1"])
+    op("V", lambda: V.tensor_scalar(T.rC[:, :], T.Jn[:, 0:64], cg(0), None, A.is_equal), r=["cG0", "Jn"], w=["rC"])
+    op("V", lambda: V.tensor_scalar(T.rL[:, 0:64], T.Jn[:, 0:64], cf(6), 64.0, A.is_equal, A.mult), r=["cF", "Jn"], w=["rL0"])
+    op("V", lambda: V.tensor_scalar(T.rL[:, 64:128], T.Jn[:, 0:64], cf(6), None, A.is_equal), r=["cF", "Jn"], w=["rL1"])
+    op("V", lambda: V.tensor_copy(T.off[:, :], T.nmI[:, :]), r=["nmI"], w=["off"])
+    for c in range(C):
+        op("V", lambda: V.tensor_scalar(T.nmC[:, 64 * c:64 * c + 64], T.nmI[:, 64 * c:64 * c + 64], cg(1), float((3 - c) * 32768), A.add, A.add),
+           r=["nmI", "cG1"], w=["nmC%d" % c])
+
+    def later_constants(part):
+        if part == 0:
+            for j, v in enumerate((1.0, -4.0, -8.0)):
+                op("V", lambda: V.memset(T.one[:, j:j + 1], v), w=["one"])
+            op("V", lambda: V.tensor_scalar(T.eyeF[:, :], T.Jn[:, :], cf(7), None, A.is_equal), r=["cF", "Jn"], w=["eyeF"])
+            for s in range(N):
+                op("V", lambda: V.tensor_scalar(T.dsel[:, 64 * s:64 * s + 64], T.Jd[:, :], float(8 * s), cf(0), A.subtract, A.is_equal),
+                   r=["Jd", "cF"], w=["dsel%d" % s])
+            return
+        op("V", lambda: V.tensor_scalar(T.dsel[:, :], T.dsel[:, :], 0.25, None, A.mult), r=["dsel%d" % s for s in range(N)], w=["dsel"])
+        op("V", lambda: V.tensor_scalar(T.quart[:, :], T.Jb[:, :], cf(0), 0.25, A.is_equal, A.mult), r=["Jb", "cF"], w=["quart"])
+        op("V", lambda: V.memset(T.tt[32:64, :], 1.0), w=["tt1"])
+
+    for s in range(N):
+        op("V", lambda: V.tensor_scalar(T.bsel[:, 128 * s:128 * s + 128], T.Jb[:, :], float(8 * s), cf(1), A.add, A.is_equal), r=["Jb", "cF"], w=["bsel%d" % s])
+    dmas("S", "lduv", turned(T.Uw, T.ue) + turned(T.Vw, T.ve), r=["qfar"], w=["Uw", "Vw"])
+    dmas("S", "ldb", sum([bias_rows(T.bias, kerows, k) for k in range(3)], []), w=["bias0", "bias1", "bias2"])
+    dmas("S", "ldx", turned(T.xB, T.x0) + turned(T.mmB, T.mm), w=["xB", "mmB"])
+
+    def q_to_psum():
+        def f():
+            PE.matmul(T.P6[:, :], T.eye[:, :], T.qa[:, 0:512], True, True)
+            return PE.matmul(T.P7[:, :], T.eye[:, :], T.qa[:, 512:1024], True, True)
+        op("P", f, r=["eye", "qown", "qfar"], w=["qP"], b=["P6", "P7"])
+
+    hmask = (cg(2), cf(4))
+    pmask = (cg(3), cf(5))
+
+    def scores(c):
+        def f():
+            for i in range(8):
+                m = PE.matmul(T.P0[:, 4 * i + c:256:32], T.prod[:, 1024 * c + i:1024 * (c + 1):8], T.rS[:, :], True, True)
+            return m
+        op("P", f, r=["prod%d" % c, "prodb%d" % c, "prodc%d" % c, "rS"], w=["S%d" % c], b=["P0"])
+
+    def gather_mul(c, a, b, tag, qs):
+        op("V", lambda: V.tensor_tensor(T.prod[:, 1024 * c + a:1024 * c + b], T.K[:, :].indirect(T.off[:, 64 * c + a // 16:64 * c + b // 16]),
+                                        T.qa[:, a:b], A.mult), r=["K", "off"] + KB + qs, w=[tag + "%d" % c])
+
+    def gather_raw(c, parts=((0, 1024),)):
+        o = (3 - c) * 1024
+        for a, b in parts:
+            op("A", lambda: S.activation(T.kraw[:, o + a:o + b], T.K[:, :].indirect(T.off[:, 64 * c + a // 16:64 * c + b // 16]), AF.Copy),
+               r=["K", "off"] + KB, w=["kraw%d" % c])
+
+    def raw_mul(c, parts=((0, 512), (512, 1024))):
+        o = (3 - c) * 1024
+        for hf, tag in ((0, "prod"), (1, "prodb")):
+            a, b = parts[hf]
+            op("V", lambda: V.tensor_tensor(T.prod[:, 1024 * c + a:1024 * c + b], T.kraw[:, o + a:o + b],
+                                            T["P%d" % (6 + hf)][:, a - 512 * hf:b - 512 * hf], A.mult),
+               r=["kraw%d" % c, "qP"], w=[tag + "%d" % c], b=["P%d" % (6 + hf)])
+
+    def names():
+        for h in range(2):
+            op("A", lambda: S.activation(T.X2[:, h::2], T.nmC[:, :], AF.Identity, scale=hmask[h]),
+               r=["nmC%d" % c for c in range(C)] + ["cG2", "cF"], w=["X2%d" % h])
+
+    def names_pe(l):
+        def f():
+            for c in range(C):
+                m = PE.matmul(T.P0[:, 256 + c:512:4], T.X2[:, 128 * c:128 * c + 128], T.rC[:, :], True, l == 0)
+                if l > 0:
+                    m = PE.matmul(T.P0[:, 256 + c:512:4], T.Xh[:, :], T.rC[:, :], False, True)
+            return m
+        op("P", f, r=["X20", "X21", "Xh0", "Xh1", "rC"], w=["code"], b=["P0"])
+
+    def select():
+        ss = ["S%d" % c for c in range(C)]
+        op("V", lambda: V.tensor_tensor_scan(T.run[:, :], T.rst[:, :], SC, 0.0, A.add, A.max), r=ss + ["rst"], w=["run"], b=["P0"])
+        op("V", lambda: V.tensor_tensor(T.old[:, 1:256], T.P0[:, 1:256], T.run[:, 0:255], A.is_le), r=ss + ["run"], w=["old"], b=["P0"])
+        op("V", lambda: V.tensor_tensor_scan(T.win[:, :], T.old[:, :], CODE, 0.0, A.mult, A.max), r=["old", "old0", "code"], w=["win"], b=["P0"])
+        op("V", lambda: V.tensor_copy(T.ci[:, :, :], T.win[:, 3::4]), r=["win"], w=["ci"])
+        op("V", lambda: V.tensor_scalar(T.DI[:, 0::2, :], T.ci[:, :, :], 6, 63, SR, AND), r=["ci"], w=["DI0"])
+        op("V", lambda: V.tensor_scalar(T.DI[:, 1::2, :], T.ci[:, :, :], 63, None, AND), r=["ci"], w=["DI1"])
+        op("V", lambda: V.tensor_copy(T.DR[:, 0], T.DI[:, :, :]), r=["DI0", "DI1"], w=["D0"])
+
+    def to_list():
+        for d in range(2):
+            for h in range(2):
+                op("A", lambda: S.activation(T.X[:, 8 * d:8 * d + 8, 8 * h:8 * h + 8], T.DR[:, 0, d::2, :], AF.Identity, scale=pmask[h]),
+                   r=["D0", "cG2", "cF"], w=["X%d%d" % (d, h)])
+            op("P", lambda: PE.matmul(LP, T.X[:, 8 * d:8 * d + 8, :], T.rL[:, 64 * d:64 * d + 64], d == 0, d == 1),
+               r=["X%d0" % d, "X%d1" % d, "rL0", "rL1"], w=["L"], b=["P2"])
+
+    def shifted():
+        for r_ in range(1, 4):
+            op("V", lambda: V.tensor_scalar(T.DR[:, r_], T.DR[:, 0], float(r_), None, A.subtract), r=["D0"], w=["D%d" % r_])
+
+    def shifted_far(n):
+        rows = slice(0, 16) if n == 4 else slice(2 * OC[1], 16)
+        op("A", lambda: S.activation(T.DR[:, n:2 * n, rows, :], T.DR[:, 0:n, rows, :], AF.Identity, bias=T.one[:, n // 4:n // 4 + 1]),
+           r=["D0", "D1", "D2", "D3", "one"] + (["D4"] if n == 8 else []), w=["D%d" % n])
+
+    def onehot(k, q0, q1):
+        for q in range(q0, q1):
+            v, n = RUNS[k][q]
+            op("V", lambda: V.tensor_scalar(T.OH[:, v:v + n, 2 * OC[k]:2 * OC[k + 1], :], T.DR[:, 0:n, 2 * OC[k]:2 * OC[k + 1], :],
+                                            float(v), None, A.is_equal), r=["D%d" % j for j in (0, 1, 2, 3, 4, 8) if j < n], w=["OH%d_%d" % (k, q)])
+
+    def counts(l, k):
+        HB = HBS[l]
+
+        def f():
+            for G in range(CH[k], CH[k + 1]):
+                j = (G - CH[k]) // 2 if l < RO - 1 else G // 2
+                o = T[HB[k]][64 * (G % 2):64 * (G % 2) + 64, 64 * j:64 * j + 64]
+                for i in range(8):
+                    m = PE.matmul(o, T.OH[:, :, 2 * G, i], T.OH[:, :, 2 * G + 1, i], i == 0, i == 7)
+            return m
+        op("P", f, r=["OH%d_%d" % (k // 2, q) for q in range(len(RUNS[k // 2]))], w=["H%d" % k], b=[HB[k]])
+
+    def new_bias(l, k):
+        HB = HBS[l]
+        cs = slice(32 * CH[k], 32 * CH[k + 1])
+        H = T[HB[k]][:, 0:32 * (CH[k + 1] - CH[k])]
+        op("V", lambda: V.tensor_scalar(H, H, 2.0, 1.0, A.min, A.subtract), r=["H%d" % k], w=["H%d" % k], b=[HB[k]])
+        op("V", lambda: V.tensor_tensor(T.bias[:, cs], T.bias[:, cs], H, A.subtract), r=["H%d" % k, "bias%d" % k], w=["bias%d" % k], b=[HB[k]])
+        rows = lambda a, b: T.K[16 * a + 15:16 * b + 16:16, :]
+        dmas("SSA"[k], "bias%d" % k, [(o, i) for i, o in bias_rows(T.bias, rows, k)], r=["bias%d" % k], w=["Kb%d" % k])
+
+    def last_bias():
+        H, hs = T.P0[:, 0:256], ["H0", "H1", "H2"]
+        op("V", lambda: V.tensor_scalar(H, H, 2.0, 1.0, A.min, A.subtract), r=hs, w=hs, b=["P0"])
+        op("V", lambda: V.tensor_tensor(T.biasF[:, :], T.bias[:, :], H, A.subtract), r=hs + ["bias0", "bias1", "bias2"], w=["biasF"], b=["P0"])
+        rows = lambda a, b: T.yb[a:b + 1, :]
+        dmas("S", "outb", [(o, i) for k in range(3) for i, o in bias_rows(T.biasF, rows, k)], r=["biasF"])
+
+    def uv_out(l, p, u):
+        o = (l * N + p) * 512 + 256 * u
+        return (T.UVl if p == rank else T.UVs)[:, o:o + 256]
+
+    def gather_uv(q, l, p, u):
+        src = (T.Uw, T.Vw)[u][:, :].indirect(T.woff[:, 16 * p:16 * p + 16])
+        fn = (lambda: V.tensor_copy(uv_out(l, p, u), src)) if q == "V" else (lambda: S.activation(uv_out(l, p, u), src, AF.Copy))
+        op(q, fn, r=["Uw", "Vw", "woff"], w=["uv%d_%d_%d" % (l, p, u)])
+
+    def have(l, s, u):
+        return ["uv%d_%d_%d" % (l, s, u)] if s == rank else ["far%d_%d" % (l, s)]
+
+    def shifts_a(l):
+        def f():
+            for s in range(N):
+                m = PE.matmul(hP, T.eyeF[:, :], T.Wl[:, 256 * l + 64 * s:256 * l + 64 * s + 64], s == 0, s == N - 1)
+            return m
+        op("P", f, r=["Wown%d" % l, "Wfar%d" % l, "eyeF"], w=["h"], b=["P0"])
+
+    def shifts_b():
+        for c in range(C):
+            op("V", lambda: V.tensor_tensor(T.tI[:, 64 * c:64 * c + 64], T.nmI[:, 64 * c:64 * c + 64], hP, A.add),
+               r=["h", "nmI"], w=["tI%d" % c], b=["P0"])
+        for h in range(2):
+            op("A", lambda: S.activation(T.Xh[:, h::2], hP, AF.Identity, scale=hmask[h]), r=["h"], w=["Xh%d" % h], b=["P0"])
+        op("V", lambda: V.tensor_scalar(T.tA[:, :], T.tI[:, :], E - 1, None, AND), r=["tI%d" % c for c in range(C)], w=["tA"])
+        op("V", lambda: V.tensor_copy(T.off[:, :], T.tA[:, :]), r=["tA"], w=["off"])
+
+    srcs = [rank] + peers[::-1]
+    dP, uP = T.P5[0:64, 0:256], T.P5[:, 256:512]
+
+    def f_prod(l, n0=0, n1=N):
+        for n in range(n0, n1):
+            s = srcs[n]
+            o = (l * N + s) * 512
+            op("V", lambda: V.tensor_tensor(T.Pf[:, 256 * s:256 * s + 256], T.UVl[:, o:o + 256], xP, A.mult), r=have(l, s, 0) + ["xP"], w=["Pf%d" % s], b=["P1"])
+            op("P", lambda: PE.matmul(dP, T.dsel[:, 64 * s:64 * s + 64], T.Pf[:, 256 * s:256 * s + 256], n == 0, n == N - 1),
+               r=["Pf%d" % s, "dsel"], w=["d"], b=["P5"])
+
+    def f_gate():
+        op("A", lambda: S.activation(T.tt[0:32, :], T.P5[0:32, 0:256], AF.Tanh, scale=2.0), r=["d"], w=["tt"], b=["P5"])
+
+    def f_silu():
+        op("V", lambda: V.tensor_tensor(T.sS[0:64, :], T.tt[0:64, :], dP, A.mult), r=["tt", "tt1", "d"], w=["sS"], b=["P5"])
+        for n, s in enumerate(srcs):
+            pb = "P%d" % (3 + n // 2)
+            op("P", lambda: PE.matmul(T[pb][:, 256 * (n % 2):256 * (n % 2) + 256], T.bsel[0:64, 128 * s:128 * s + 128], T.sS[0:64, :], True, True),
+               r=["sS", "bsel%d" % s], w=["B%d" % s], b=[pb])
+
+    def mix(l, n):
+        mm = T.mmF[:, 16:144] if l == RO - 1 else T.mmF[:, 0:128]
+        if n < 0:
+            op("P", lambda: PE.matmul(uP, mm, T.xS[:, :], True, False), r=["mmF0", "mmF1", "xS"], w=["u"], b=["P5"])
+        else:
+            s = srcs[n]
+            op("P", lambda: PE.matmul(uP, mm, T.Yf[:, 256 * s:256 * s + 256], False, n == N - 1), r=["Yf%d" % s], w=["u"], b=["P5"])
+
+    def f_y(l, n0, n1):
+        for n in range(n0, n1):
+            s = srcs[n]
+            pb = "P%d" % (3 + n // 2)
+            o = (l * N + s) * 512 + 256
+            op("V", lambda: V.tensor_tensor(T.Yf[:, 256 * s:256 * s + 256], T.UVl[:, o:o + 256], T[pb][:, 256 * (n % 2):256 * (n % 2) + 256], A.mult),
+               r=have(l, s, 1) + ["B%d" % s], w=["Yf%d" % s], b=[pb])
+            mix(l, n)
+
+    FB = ("P3", "P4", "P6", "P7")
+
+    def last_a(n):
+        s, pb, l = srcs[n], FB[n], RO - 1
+        o, cs = (l * N + s) * 512, slice(256 * s, 256 * s + 256)
+        op("V", lambda: V.tensor_tensor(T.Pf[:, cs], T.UVl[:, o:o + 256], xP, A.mult), r=have(l, s, 0) + ["xP"], w=["Pf%d" % s], b=["P1"])
+        op("P", lambda: PE.matmul(T[pb][:, 0:256], T.quart[:, :], T.Pf[:, cs], True, True), r=["Pf%d" % s, "quart"], w=["dl%d" % s], b=[pb])
+        op("A", lambda: S.activation(T.t4[:, cs], T[pb][:, 0:256], AF.Tanh, scale=2.0), r=["dl%d" % s], w=["t4%d" % s], b=[pb])
+        op("A", lambda: S.activation(T[pb][:, 256:512], T.t4[:, cs], AF.Identity, bias=T.one[:, 0:1]), r=["t4%d" % s, "one"], w=["t5%d" % s], b=[pb])
+
+    def last_b(n):
+        s, pb, l = srcs[n], FB[n], RO - 1
+        o, cs = (l * N + s) * 512 + 256, slice(256 * s, 256 * s + 256)
+        op("V", lambda: V.tensor_tensor(T.Pf[:, cs], T.UVl[:, o:o + 256], T[pb][:, 0:256], A.mult), r=have(l, s, 1) + ["dl%d" % s], w=["Pf%d" % s], b=[pb])
+        op("V", lambda: V.tensor_tensor(T.Yf[:, cs], T.Pf[:, cs], T[pb][:, 256:512], A.mult), r=["Pf%d" % s, "t5%d" % s], w=["Yf%d" % s], b=[pb])
+        mix(l, n)
+
+    def f_tanh(l):
+        if l < RO - 1:
+            op("A", lambda: S.activation(xP, uP, AF.Tanh, scale=0.5), r=["u"], w=["xP"], b=["P5", "P1"])
+            op("A", lambda: S.activation(T.xS[:, :], uP, AF.Tanh, scale=0.5), r=["u"], w=["xS"], b=["P5"])
+        else:
+            op("A", lambda: S.activation(T.xo[:, :], uP, AF.Tanh, scale=0.5), r=["u"], w=["xo"], b=["P5"])
+            dmas("A", "outx", [(T.yx[:, :], T.xo[:, :])], r=["xo"])
+
+    def x_start():
+        op("A", lambda: S.activation(xP, T.xB[:, :], AF.Copy), r=["xB"], w=["xP"], b=["P1"])
+        op("A", lambda: S.activation(T.xS[:, :], T.xB[:, :], AF.Copy), r=["xB"], w=["xS"])
+        op("A", lambda: S.activation(T.mmF[:, 16:144], T.mmB[:, :], AF.Copy), r=["mmB"], w=["mmF0"])
+        op("A", lambda: S.activation(T.mmF[:, 0:16], T.mmB[:, 112:128], AF.Copy), r=["mmB"], w=["mmF1"])
+
+    for l in range(RO):
+        last = l == RO - 1
+        if l == 0:
+            names()
+            names_pe(0)
+            a, b = rank * TK, (rank + 1) * TK
+            far = [(x if x != a else b, x + 512 if x + 512 != b else a) for x in (0, 512)]
+            for c in (3, 2, 1):
+                gather_raw(c, far)
+            for c in range(C):
+                gather_mul(c, a, b, "prodc", ["qown"])
+            later_constants(0)
+            q_to_psum()
+            gather_mul(0, far[0][0], far[0][1], "prod", ["qfar"])
+            gather_mul(0, far[1][0], far[1][1], "prodb", ["qfar"])
+            scores(0)
+            for c in (3, 2, 1):
+                raw_mul(c, far)
+                scores(c)
+        elif l == 1:
+            gather_raw(3)
+            gather_raw(2)
+            x_start()
+            for c in range(2):
+                gather_mul(c, 0, 1024, "prod", ["qown", "qfar"])
+                if c == 0:
+                    names_pe(l)
+                scores(c)
+            for c in (3, 2):
+                raw_mul(c)
+                scores(c)
+        else:
+            gather_raw(3)
+            f_gate()
+            gather_raw(2)
+            gather_raw(1)
+            gather_mul(0, 0, 1024, "prod", ["qown", "qfar"])
+            names_pe(l)
+            scores(0)
+            mix(l - 2, -1)
+            raw_mul(3)
+            scores(3)
+            f_silu()
+            raw_mul(2)
+            scores(2)
+            f_y(l - 2, 0, 2)
+            raw_mul(1)
+            scores(1)
+            f_y(l - 2, 2, 4)
+            f_tanh(l - 2)
+        select()
+        to_list()
+        if not last:
+            wo = T.Wl[:, 256 * l + 64 * rank:256 * l + 64 * rank + 64]
+            shifted()
+            shifted_far(4)
+            op("A", lambda: S.activation(wo, LP, AF.Copy), r=["L"], w=["Wown%d" % l], b=["P2"])
+            to_all(wo, "arrW%d" % l, ["Wown%d" % l])
+            arrives("arrW%d" % l, 3 * len(eng), "Wfar%d" % l)
+            shifted_far(8)
+            onehot(0, 0, 5)
+            op("V", lambda: V.tensor_copy(T.woff[:, :], wo), r=["Wown%d" % l], w=["woff"])
+            for p in peers + [rank]:
+                gather_uv("A", l, p, 0)
+                gather_uv("A", l, p, 1)
+            onehot(0, 5, len(RUNS[0]))
+            counts(l, 0)
+            counts(l, 1)
+            onehot(1, 0, 3)
+            new_bias(l, 0)
+            onehot(1, 3, 4)
+            counts(l, 2)
+            shifts_a(l)
+            new_bias(l, 1)
+            if l > 0:
+                f_prod(l - 1, 0, 1)
+            new_bias(l, 2)
+            if l > 0:
+                f_prod(l - 1, 1, 2)
+            shifts_b()
+            if l > 0:
+                f_prod(l - 1, 2, 4)
+            else:
+                later_constants(1)
+            for k in range(N - 1):
+                to_home(l, k, KB)
+        else:
+            f_prod(l - 1, 0, 1)
+            shifted()
+            shifted_far(4)
+            f_prod(l - 1, 1, 3)
+            op("V", lambda: V.tensor_copy(T.woff[:, :], LP), r=["L"], w=["woff"], b=["P2"])
+            f_prod(l - 1, 3, 4)
+            mix(l - 1, -1)
+            for k, p in enumerate(peers):
+                gather_uv("V" if k == 0 else "A", l, p, 0)
+                gather_uv("A", l, p, 1)
+                to_home(l, k, [])
+                if k == 1:
+                    f_gate()
+            shifted_far(8)
+            gather_uv("A", l, rank, 0)
+            gather_uv("A", l, rank, 1)
+            onehot(0, 0, 5)
+            f_silu()
+            onehot(0, 5, 7)
+            f_y(l - 1, 0, 2)
+            onehot(0, 7, 8)
+            f_y(l - 1, 2, 4)
+            f_tanh(l - 1)
+            onehot(0, 8, 10)
+            counts(l, 0)
+            onehot(1, 0, 4)
+            last_a(0)
+            last_a(1)
+            last_a(2)
+            last_a(3)
+            counts(l, 1)
+            counts(l, 2)
+            mix(l, -1)
+            last_b(0)
+            last_b(1)
+            last_b(2)
+            last_bias()
+            last_b(3)
+            f_tanh(l)
+    for s in total:
+        if max(seen[q].get(s, 0) for q in Q) < total[s]:
+            need("G", (s, total[s]))

@@ -2,37 +2,42 @@ from concourse.bass import DstId, RemoteDMATransfer
 from concourse.mybir import AluOpType, ActivationFunctionType
 
 N, E, TK, C, RO = 4, 4096, 256, 4, 4
-REP = 16
-RUNS = ([(v, 4) for v in range(0, 16, 4)] + [(v, 8) for v in range(16, 64, 8)], [(v, 16) for v in range(0, 64, 16)])
-OC = (0, 6, 8)
-CH = (0, 4, 6, 8)
+REP = 8
 F32, BF, I32, U16, F16 = "float32", "bfloat16", "int32", "uint16", "float16"
+MID = [("V", 0, 1, "P1"), ("V", 1, 2, "P2"), ("V", 2, 3, "P1"), ("A", 3, 4, "P0")]
+END = [("V", 0, 2, "P0"), ("V", 2, 4, "P2")]
+HC = {"P0": 384, "P1": 0, "P2": 0}
+FILL = (1, 2, 0, 3)
+RAW = [(3, 0, 512), (3, 512, 1024), (2, 0, 512), (2, 512, 1024), (1, 512, 1024), (1, 256, 512)]
 
 SCRATCH = {
     "K": ("sbuf", [128, E], BF), "Uw": ("sbuf", [128, E], BF), "Vw": ("sbuf", [128, E], BF),
-    "nmI": ("sbuf", [128, 256], I32), "nmC": ("sbuf", [128, 256], F32), "qa": ("sbuf", [128, 1024], BF),
-    "off": ("sbuf", [128, 256], U16), "woff": ("sbuf", [128, 64], U16),
-    "prod": ("sbuf", [128, 4096], F16), "kraw": ("sbuf", [128, 3072], BF),
-    "tI": ("sbuf", [128, 256], I32), "tA": ("sbuf", [128, 256], I32),
-    "Xh": ("sbuf", [128, 128], F32), "eyeF": ("sbuf", [128, 128], F32), "X2": ("sbuf", [128, 512], F32),
+    "nmI": ("sbuf", [128, 256], I32), "nmC": ("sbuf", [128, 256], F32), "nmH": ("sbuf", [128, 256], F16), "qa": ("sbuf", [128, 1024], BF),
+    "off": ("sbuf", [128, 256], U16), "woff": ("sbuf", [128, 64], U16), "tI": ("sbuf", [128, 256], I32), "tA": ("sbuf", [128, 256], I32),
+    "prod": ("sbuf", [128, 4096], F16), "kraw": ("sbuf", [128, 4096], BF),
+    "Xh": ("sbuf", [128, 128], F32), "X2": ("sbuf", [128, 512], F32), "nameT": ("sbuf", [128, 256], F32),
     "run": ("sbuf", [128, 256], F32), "old": ("sbuf", [128, 256], F32), "win": ("sbuf", [128, 256], F32),
-    "rst": ("sbuf", [128, 256], F32), "ci": ("sbuf", [128, 8, 8], I32), "DI": ("sbuf", [128, 16, 8], I32),
-    "DR": ("sbuf", [128, REP, 16, 8], BF), "X": ("sbuf", [128, 16, 16], BF), "OH": ("sbuf", [128, 64, 16, 8], BF),
-    "bias": ("sbuf", [128, 256], BF), "biasF": ("sbuf", [128, 256], F32),
-    "Wl": ("sbuf", [128, 3 * 256], F32), "UVs": ("sbuf", [128, RO * N * 512], BF), "UVl": ("sbuf", [128, RO * N * 512], BF),
+    "rst": ("sbuf", [128, 256], F32), "ci": ("sbuf", [128, 8, 8], I32), "DI": ("sbuf", [128, 64, 2], I32),
+    "DR": ("sbuf", [128, REP, 128], BF), "X": ("sbuf", [128, 8, 32], BF), "OH": ("sbuf", [128, 65, 128], BF),
+    "bias": ("sbuf", [128, 256], BF), "nb": ("sbuf", [128, 256], BF), "nb2": ("sbuf", [128, 256], BF),
+    "nbF": ("sbuf", [128, 256], F32), "biasF": ("sbuf", [128, 256], F32), "Ss": ("sbuf", [128, 128], F32),
+    "Wl": ("sbuf", [128, 3 * 256], F16), "UVs": ("sbuf", [128, RO * N * 512], BF), "UVl": ("sbuf", [128, RO * N * 512], BF),
     "xB": ("sbuf", [128, 256], BF), "xS": ("sbuf", [128, 256], F32), "xo": ("sbuf", [128, 256], F32),
     "mmB": ("sbuf", [128, 128], BF), "mmF": ("sbuf", [128, 144], F32),
-    "Pf": ("sbuf", [128, 1024], F32), "Yf": ("sbuf", [128, 1024], F32), "tt": ("sbuf", [128, 256], F32), "sS": ("sbuf", [128, 256], F32),
-    "pI": ("sbuf", [128, 2], I32), "cI": ("sbuf", [128, 8], I32), "cF": ("sbuf", [128, 8], F32), "cG": ("sbuf", [128, 8], F32),
-    "Jn": ("sbuf", [128, 128], F32), "Jd": ("sbuf", [128, 64], F32), "Jb": ("sbuf", [128, 128], F32),
-    "rS": ("sbuf", [128, 8], F16), "rC": ("sbuf", [128, 64], F32), "rL": ("sbuf", [128, 128], BF), "eye": ("sbuf", [128, 128], BF),
-    "quart": ("sbuf", [128, 128], F32), "t4": ("sbuf", [128, 1024], F32), "one": ("sbuf", [128, 4], F32),
-    "dsel": ("sbuf", [128, 256], F32), "bsel": ("sbuf", [128, 512], F32),
+    "Pf": ("sbuf", [128, 1024], F32), "Yf": ("sbuf", [128, 1024], F32), "tt": ("sbuf", [128, 128], F32), "sS": ("sbuf", [128, 128], F32),
+    "pI": ("sbuf", [128, 2], I32), "cI": ("sbuf", [128, 12], I32), "cF": ("sbuf", [128, 12], F32), "cG": ("sbuf", [128, 12], F32),
+    "Jn": ("sbuf", [128, 128], F32), "Jd": ("sbuf", [128, 192], F32), "Jb": ("sbuf", [128, 128], F32),
+    "rS": ("sbuf", [128, 16], F16), "rC": ("sbuf", [128, 64], F32), "rL": ("sbuf", [128, 128], BF),
+    "eye": ("sbuf", [128, 128], BF), "eyeH": ("sbuf", [128, 128], F16),
+    "Da": ("sbuf", [128, 128], F32), "Db": ("sbuf", [128, 128], F32), "Dp": ("sbuf", [128, 128], F32), "Dn": ("sbuf", [128, 128], F32),
+    "quart": ("sbuf", [128, 128], F32), "t4": ("sbuf", [128, 1024], F32),
+    "con": ("sbuf", [128, 16], F32), "dsel": ("sbuf", [128, 192], F32), "bsel": ("sbuf", [128, 1024], F32),
 }
 for _b in range(8):
     SCRATCH["P%d" % _b] = ("psum", [128, 512], F32)
-SEMAPHORES = (["cV", "cA", "cP", "cG", "ldq", "ldn", "ldk", "ldb", "ldx", "lduv", "bias0", "bias1", "bias2", "outb", "outx", "sent", "arrq"]
-              + ["arrW%d" % l for l in range(RO - 1)] + ["arrU%d_%d" % (l, k) for l in range(RO) for k in range(N - 1)])
+SEMAPHORES = (["cV", "cA", "cP", "cG", "ldq", "ldn", "ldk", "ldb", "ldx", "lduv", "bias0", "bias1", "bias2", "bias3", "outb", "outx", "sent", "sentq"]
+              + ["arrq%d" % s for s in range(N)] + ["arrW%d_%d" % (l, s) for l in range(RO - 1) for s in range(N)]
+              + ["arrU%d_%d_%d" % (l, s, u) for l in range(RO) for s in range(N) for u in range(2)])
 
 
 def rank_program(g, core, T, topo):
@@ -91,6 +96,7 @@ def rank_program(g, core, T, topo):
         lastw[w] = [(sem, total[sem], "far")]
 
     peers = [(rank + k) % N for k in range(1, N)]
+    srcs = [rank] + peers[::-1]
     eng = [e for e in topo.engines(core, T.cores[peers[0]]) if all(e in topo.engines(core, T.cores[p]) for p in peers)]
     assert all(topo.may_write(core, T.cores[p]) for p in peers) and len(eng) >= 8
     eng = eng[:8]
@@ -102,249 +108,349 @@ def rank_program(g, core, T, topo):
         a = topo.addr(T.cores[p])
         return DstId(rid=a[0], pnc=a[1])
 
-    def to_all(ap, sem, r):
+    def to_all(ap, sem, r, name, left="sent"):
         order("G", r, (), (), True)
-        g.remote_dma_fused([RemoteDMATransfer(dst_ids=[dst(p) for p in peers], dma_engine_mask=bits(eng), remote_sem=T.sem[sem],
-                                              srcs=[ap], dsts=[ap] * len(peers))], local_sem=T.sem.sent)
-        total["sent"] = total.get("sent", 0) + len(eng)
+        g.remote_dma_fused([RemoteDMATransfer(dst_ids=[dst(p) for p in peers], dma_engine_mask=bits(eng), remote_sem=T.sem[sem % rank],
+                                              srcs=[ap], dsts=[ap] * len(peers))], local_sem=T.sem[left])
+        total[left] = total.get(left, 0) + len(eng)
+        for p in peers:
+            arrives(sem % p, len(eng), name % p)
 
-    def to_home(l, k, more):
-        p = peers[k]
-        order("G", ["uv%d_%d_0" % (l, p), "uv%d_%d_1" % (l, p)] + more, (), (), True)
-        so, do = (l * N + p) * 512, (l * N + rank) * 512
-        g.remote_dma_fused([RemoteDMATransfer(dst_ids=[dst(p)], dma_engine_mask=bits(eng), remote_sem=T.sem["arrU%d_%d" % (l, k)],
-                                              src=T.UVs[:, so:so + 512], dst=T.UVl[:, do:do + 512])], local_sem=T.sem.sent)
-        total["sent"] = total.get("sent", 0) + len(eng)
-        arrives("arrU%d_%d" % (l, k), len(eng), "far%d_%d" % (l, (rank - k - 1) % N))
+    def to_home(l, parts, more=()):
+        es = [eng[j::len(parts)] for j in range(len(parts))]
+        trs = []
+        for (k, u0, u1), e in zip(parts, es):
+            p, s = peers[k], (rank - k - 1) % N
+            order("G", ["uv%d_%d_%d" % (l, p, u) for u in range(u0, u1)] + list(more), (), (), True)
+            so, do = (l * N + p) * 512, (l * N + rank) * 512
+            trs.append(RemoteDMATransfer(dst_ids=[dst(p)], dma_engine_mask=bits(e), remote_sem=T.sem["arrU%d_%d_%d" % (l, rank, u0)],
+                                         src=T.UVs[:, so + 256 * u0:so + 256 * u1], dst=T.UVl[:, do + 256 * u0:do + 256 * u1]))
+            total["sent"] = total.get("sent", 0) + len(e)
+            arrives("arrU%d_%d_%d" % (l, s, u0), len(e), "far%d_%d_%d" % (l, s, u0))
+            for u in range(u0 + 1, u1):
+                lastw["far%d_%d_%d" % (l, s, u)] = lastw["far%d_%d_%d" % (l, s, u0)]
+        g.remote_dma_fused(trs, local_sem=T.sem.sent)
 
     V, S, PE = g.vector, g.scalar, g.tensor
-    SC, CODE = T.P0[:, 0:256], T.P0[:, 256:512]
-    HBS = [("P1", "P2", "P3")] * (RO - 1) + [("P0", "P0", "P0")]
-    KB = ["Kb0", "Kb1", "Kb2"]
-    xP, LP, hP = T.P1[:, 256:512], T.P2[:, 128:192], T.P0[:, 0:64]
+    SC, hT, LP, hP = T.P0[:, 0:256], T.P0[:, 256:320], T.P0[:, 320:384], T.P0[:, 0:64]
+    xP, yP = T.P1[:, 256:512], T.P2[:, 128:384]
+    dP, uP = T.P5[:, 0:128], T.P5[:, 256:512]
+    KB, NB, QS = ["Kb%d" % j for j in range(4)], ["nb%d" % j for j in range(4)], ["q%d" % s for s in range(N)]
 
     def turned(d, s):
         return [(d[16:128, :], s[0:112, :]), (d[0:16, :], s[112:128, :])]
 
-    def bias_rows(t, rows, k):
+    def bias_rows(t, rows, j0, j1):
         out = []
-        for j in range(CH[k] // 2, CH[k + 1] // 2):
+        for j in range(j0, j1):
             if j == 0:
                 out += [(t[0:64, 0:64], rows(7, 7)), (t[64:128, 0:64], rows(0, 0))]
             else:
                 out.append((t[:, 64 * j:64 * j + 64], rows(2 * j - 1, 2 * j)))
         return out
 
-    own = slice(rank * TK, (rank + 1) * TK)
-    dmas("S", "ldq", [(T.qa[:, own], T.rq[:, :])], w=["qown"])
+    blk = lambda s: slice(s * TK, (s + 1) * TK)
+    dmas("S", "ldq", [(T.qa[:, blk(rank)], T.rq[:, :])], w=["q%d" % rank])
     dmas("S", "ldk", [(T.K[:, :], T.ke[:, :])], w=["K"])
     dmas("A", "ldn", [(T.nmI[:, :], T.nm[:, :])], w=["nmI"])
     kerows = lambda a, b: T.ke[16 * a + 15:16 * b + 16:16, :]
+    flt = dict(allow_small_or_imprecise_dtypes=True)
     op("G", lambda: g.iota(T.pI[:, :], [[16, 2]], 0, 1), w=["pI"])
-    op("G", lambda: g.iota(T.Jn[:, :], [[1, 128]], 0, 0, allow_small_or_imprecise_dtypes=True), w=["Jn"])
-    op("G", lambda: g.iota(T.Jb[:, :], [[1, 8], [0, 16]], 0, 0, allow_small_or_imprecise_dtypes=True), w=["Jb"])
-    to_all(T.qa[:, own], "arrq", ["qown"])
-    arrives("arrq", 3 * len(eng), "qfar")
-    op("G", lambda: g.iota(T.Jd[:, :], [[0, 2], [1, 32]], 0, 0, allow_small_or_imprecise_dtypes=True), w=["Jd"])
+    op("G", lambda: g.iota(T.Jn[:, :], [[1, 128]], 0, 0, **flt), w=["Jn"])
+    op("G", lambda: g.iota(T.Jb[:, :], [[1, 8], [0, 16]], 0, 0, **flt), w=["Jb"])
+    op("G", lambda: g.iota(T.Jd[:, :], [[0, 3], [1, 64]], 0, 0, **flt), w=["Jd"])
+    to_all(T.qa[:, blk(rank)], "arrq%d", ["q%d" % rank], "q%d", "sentq")
+    lastw["qleft"] = [("sentq", total["sentq"], "far")]
     SR, AND = A.arith_shift_right, A.bitwise_and
     p0, p16 = T.pI[:, 0:1], T.pI[:, 1:2]
-    for j, (src, sh, m) in enumerate([(p0, 4, 7), (p0, 0, 31), (p0, 0, 7), (p16, 4, 7), (p0, 3, 1), (p0, 0, 1), (p0, 1, 63), (p0, 0, 127)]):
-        op("V", lambda: V.tensor_scalar(T.cI[:, j:j + 1], src, sh, m, SR, AND), r=["pI"], w=["cI%d" % j])
-    op("V", lambda: V.memset(T.rst[:, :], 0.0), w=["rst0"])
-    op("V", lambda: V.tensor_copy(T.cF[:, :], T.cI[:, :]), r=["cI%d" % j for j in range(8)], w=["cF"])
-    op("V", lambda: V.memset(T.rst[:, 0::4], -100000.0), r=["rst0"], w=["rst"])
-    op("V", lambda: V.memset(T.old[:, 0:1], 0.0), w=["old0"])
     cf = lambda j: T.cF[:, j:j + 1]
     cg = lambda j: T.cG[:, j:j + 1]
+    con = lambda j: T.con[:, j:j + 1]
+    for j, v in ((10, 20.0), (8, 2.0), (9, 4.0), (12, -4.0), (13, 1.0)):
+        op("V", lambda: V.memset(con(j), v), w=["con%d" % j])
+    op("A", lambda: S.activation(T.tt[64:128, :], T.Jn[64:128, :], AF.Tanh, bias=T.con[64:128, 10:11]), r=["Jn", "con10"], w=["tt1"])
+    cols = [(p0, 4, 7), (p0, 0, 63), (p0, 0, 7), (p16, 4, 7), (p0, 3, 1), (p0, 0, 1), (p0, 1, 63), (p0, 0, 127), (p0, 0, 15)]
+    for j, (src, sh, m) in enumerate(cols):
+        op("V", lambda: V.tensor_scalar(T.cI[:, j:j + 1], src, sh, m, SR, AND), r=["pI"], w=["cI%d" % j])
+    op("V", lambda: V.tensor_copy(T.cF[:, 0:9], T.cI[:, 0:9]), r=["cI%d" % j for j in range(9)], w=["cF"])
+    op("V", lambda: V.memset(T.old[:, 0:1], 0.0), w=["old0"])
     op("V", lambda: V.tensor_scalar(cg(0), cf(3), 8.0, cf(2), A.mult, A.add), r=["cF"], w=["cG0"])
     op("V", lambda: V.tensor_scalar(T.cG[:, 2:4], T.cF[:, 4:6], 0.0, None, A.is_equal), r=["cF"], w=["cG2"])
-    op("V", lambda: V.tensor_scalar(T.rS[:, :], T.Jn[:, 0:8], cf(3), None, A.is_equal), r=["cF", "Jn"], w=["rS"])
-    op("V", lambda: V.tensor_scalar(T.eye[:, :], T.Jn[:, :], cf(7), None, A.is_equal), r=["cF", "Jn"], w=["eye"])
     op("V", lambda: V.tensor_scalar(cg(1), cg(0), 131072.0, None, A.mult), r=["cG0"], w=["cG1"])
     op("V", lambda: V.tensor_scalar(T.rC[:, :], T.Jn[:, 0:64], cg(0), None, A.is_equal), r=["cG0", "Jn"], w=["rC"])
-    op("V", lambda: V.tensor_scalar(T.rL[:, 0:64], T.Jn[:, 0:64], cf(6), 64.0, A.is_equal, A.mult), r=["cF", "Jn"], w=["rL0"])
-    op("V", lambda: V.tensor_scalar(T.rL[:, 64:128], T.Jn[:, 0:64], cf(6), None, A.is_equal), r=["cF", "Jn"], w=["rL1"])
     op("V", lambda: V.tensor_copy(T.off[:, :], T.nmI[:, :]), r=["nmI"], w=["off"])
     for c in range(C):
-        op("V", lambda: V.tensor_scalar(T.nmC[:, 64 * c:64 * c + 64], T.nmI[:, 64 * c:64 * c + 64], cg(1), float((3 - c) * 32768), A.add, A.add),
+        op("V", lambda: V.tensor_scalar(T.nmC[:, 64 * c:64 * c + 64], T.nmI[:, 64 * c:64 * c + 64], cg(1), float((3 - c) * 32768 + 8192), A.add, A.add),
            r=["nmI", "cG1"], w=["nmC%d" % c])
+    op("V", lambda: V.tensor_scalar(T.eye[:, :], T.Jn[:, :], cf(7), None, A.is_equal), r=["cF", "Jn"], w=["eye"])
+    op("V", lambda: V.memset(T.rst[:, :], 0.0), w=["rst0"])
+    op("V", lambda: V.tensor_scalar(T.rS[:, 0:8], T.Jn[:, 0:8], cf(3), None, A.is_equal), r=["cF", "Jn"], w=["rS0"])
+    op("V", lambda: V.memset(T.rst[:, 0::4], -100000.0), r=["rst0"], w=["rst"])
+    op("V", lambda: V.tensor_scalar(T.rL[:, 0:64], T.Jn[:, 0:64], cf(6), 64.0, A.is_equal, A.mult), r=["cF", "Jn"], w=["rL0"])
+    op("V", lambda: V.tensor_scalar(T.rL[:, 64:128], T.Jn[:, 0:64], cf(6), None, A.is_equal), r=["cF", "Jn"], w=["rL1"])
+    op("V", lambda: V.tensor_scalar(T.con[:, 0:8], T.Jn[:, 0:8], -float(REP), 0.5, A.mult, A.add), r=["Jn"], w=["con0"])
 
-    def later_constants(part):
-        if part == 0:
-            for j, v in enumerate((1.0, -4.0, -8.0)):
-                op("V", lambda: V.memset(T.one[:, j:j + 1], v), w=["one"])
-            op("V", lambda: V.tensor_scalar(T.eyeF[:, :], T.Jn[:, :], cf(7), None, A.is_equal), r=["cF", "Jn"], w=["eyeF"])
-            for s in range(N):
-                op("V", lambda: V.tensor_scalar(T.dsel[:, 64 * s:64 * s + 64], T.Jd[:, :], float(8 * s), cf(0), A.subtract, A.is_equal),
-                   r=["Jd", "cF"], w=["dsel%d" % s])
+    def count_constants(part):
+        if part == 1:
+            op("V", lambda: V.tensor_scalar(T.nmH[:, :], T.nmI[:, :], 2048.0, None, A.subtract), r=["nmI"], w=["nmH"])
+            op("V", lambda: V.tensor_scalar(T.eyeH[:, :], T.eye[:, :], 1.0, None, A.mult), r=["eye"], w=["eyeH"])
+            op("V", lambda: V.memset(T.OH[:, 64], -1.0), w=["OHend"])
+            op("V", lambda: V.tensor_scalar(T.rS[:, 8:16], T.Jn[:, 0:8], cf(3), cg(7), A.is_equal, A.mult), r=["cF", "Jn", "cG7"], w=["rS1"])
             return
-        op("V", lambda: V.tensor_scalar(T.dsel[:, :], T.dsel[:, :], 0.25, None, A.mult), r=["dsel%d" % s for s in range(N)], w=["dsel"])
-        op("V", lambda: V.tensor_scalar(T.quart[:, :], T.Jb[:, :], cf(0), 0.25, A.is_equal, A.mult), r=["Jb", "cF"], w=["quart"])
-        op("V", lambda: V.memset(T.tt[32:64, :], 1.0), w=["tt1"])
+        op("V", lambda: V.tensor_scalar(cg(4), cf(1), 0.0, 0.25, A.is_equal, A.mult), r=["cF"], w=["cG4"])
+        op("V", lambda: V.tensor_scalar(cg(5), cf(1), 0.0, -0.25, A.not_equal, A.mult), r=["cF"], w=["cG5"])
+        op("V", lambda: V.tensor_scalar(cg(8), cf(7), 1.0, None, A.subtract), r=["cF"], w=["cG8"])
+        op("V", lambda: V.tensor_scalar(cg(9), cf(7), 63.0, None, A.add), r=["cF"], w=["cG9"])
+        op("V", lambda: V.tensor_scalar(cg(6), cf(8), 15.0, -2.0, A.is_equal, A.mult), r=["cF"], w=["cG6"])
+        op("V", lambda: V.tensor_scalar(T.Da[:, :], T.Jn[:, :], cg(8), cg(5), A.is_equal, A.mult), r=["Jn", "cG8", "cG5"], w=["Da"])
+        op("V", lambda: V.tensor_scalar(T.Db[:, :], T.Jn[:, :], cg(9), cg(4), A.is_equal, A.mult), r=["Jn", "cG9", "cG4"], w=["Db"])
+        op("V", lambda: V.tensor_scalar(T.Dn[:, :], T.Jn[:, :], cf(7), 0.25, A.is_equal, A.mult), r=["Jn", "cF"], w=["Dq"])
+        op("V", lambda: V.tensor_scalar(cg(7), cg(6), 1.0, None, A.add), r=["cG6"], w=["cG7"])
+        op("V", lambda: V.tensor_tensor(T.Da[:, :], T.Da[:, :], T.Db[:, :], A.add), r=["Da", "Db"], w=["Da"])
+        op("V", lambda: V.tensor_tensor(T.Dp[:, :], T.Da[:, :], T.Dn[:, :], A.add), r=["Da", "Dq"], w=["Dp"])
+        op("V", lambda: V.tensor_scalar(T.Dn[:, :], T.Dp[:, :], -1.0, None, A.mult), r=["Dp"], w=["Dn"])
 
-    for s in range(N):
-        op("V", lambda: V.tensor_scalar(T.bsel[:, 128 * s:128 * s + 128], T.Jb[:, :], float(8 * s), cf(1), A.add, A.is_equal), r=["Jb", "cF"], w=["bsel%d" % s])
-    dmas("S", "lduv", turned(T.Uw, T.ue) + turned(T.Vw, T.ve), r=["qfar"], w=["Uw", "Vw"])
-    dmas("S", "ldb", sum([bias_rows(T.bias, kerows, k) for k in range(3)], []), w=["bias0", "bias1", "bias2"])
+    def x_constants(part):
+        if part == 0:
+            op("V", lambda: V.tensor_scalar(cg(10), cf(0), 56.0, None, A.add), r=["cF"], w=["cG10"])
+            op("V", lambda: V.tensor_scalar(T.quart[:, :], T.Jb[:, :], cf(0), 0.25, A.is_equal, A.mult), r=["Jb", "cF"], w=["quart"])
+            op("V", lambda: V.tensor_scalar(T.dsel[:, :], T.Jd[:, :], cg(10), 0.25, A.is_equal, A.mult), r=["Jd", "cG10"], w=["dsel"])
+            return
+        for k in range(4 * part - 4, 4 * part):
+            op("V", lambda: V.tensor_scalar(T.bsel[:, 128 * k:128 * k + 128], T.Jb[:, :], float(8 * k), cf(1), A.add, A.is_equal), r=["Jb", "cF"], w=["bsel%d" % k])
+
+    dmas("S", "ldb", bias_rows(T.bias, kerows, 0, 4), r=["qleft"], w=["bias"])
+    dmas("S", "lduv", turned(T.Uw, T.ue) + turned(T.Vw, T.ve), w=["Uw", "Vw"])
     dmas("S", "ldx", turned(T.xB, T.x0) + turned(T.mmB, T.mm), w=["xB", "mmB"])
-
-    def q_to_psum():
-        def f():
-            PE.matmul(T.P6[:, :], T.eye[:, :], T.qa[:, 0:512], True, True)
-            return PE.matmul(T.P7[:, :], T.eye[:, :], T.qa[:, 512:1024], True, True)
-        op("P", f, r=["eye", "qown", "qfar"], w=["qP"], b=["P6", "P7"])
 
     hmask = (cg(2), cf(4))
     pmask = (cg(3), cf(5))
-
-    def scores(c):
-        def f():
-            for i in range(8):
-                m = PE.matmul(T.P0[:, 4 * i + c:256:32], T.prod[:, 1024 * c + i:1024 * (c + 1):8], T.rS[:, :], True, True)
-            return m
-        op("P", f, r=["prod%d" % c, "prodb%d" % c, "prodc%d" % c, "rS"], w=["S%d" % c], b=["P0"])
-
-    def gather_mul(c, a, b, tag, qs):
-        op("V", lambda: V.tensor_tensor(T.prod[:, 1024 * c + a:1024 * c + b], T.K[:, :].indirect(T.off[:, 64 * c + a // 16:64 * c + b // 16]),
-                                        T.qa[:, a:b], A.mult), r=["K", "off"] + KB + qs, w=[tag + "%d" % c])
-
-    def gather_raw(c, parts=((0, 1024),)):
-        o = (3 - c) * 1024
-        for a, b in parts:
-            op("A", lambda: S.activation(T.kraw[:, o + a:o + b], T.K[:, :].indirect(T.off[:, 64 * c + a // 16:64 * c + b // 16]), AF.Copy),
-               r=["K", "off"] + KB, w=["kraw%d" % c])
-
-    def raw_mul(c, parts=((0, 512), (512, 1024))):
-        o = (3 - c) * 1024
-        for hf, tag in ((0, "prod"), (1, "prodb")):
-            a, b = parts[hf]
-            op("V", lambda: V.tensor_tensor(T.prod[:, 1024 * c + a:1024 * c + b], T.kraw[:, o + a:o + b],
-                                            T["P%d" % (6 + hf)][:, a - 512 * hf:b - 512 * hf], A.mult),
-               r=["kraw%d" % c, "qP"], w=[tag + "%d" % c], b=["P%d" % (6 + hf)])
 
     def names():
         for h in range(2):
             op("A", lambda: S.activation(T.X2[:, h::2], T.nmC[:, :], AF.Identity, scale=hmask[h]),
                r=["nmC%d" % c for c in range(C)] + ["cG2", "cF"], w=["X2%d" % h])
 
-    def names_pe(l):
         def f():
             for c in range(C):
-                m = PE.matmul(T.P0[:, 256 + c:512:4], T.X2[:, 128 * c:128 * c + 128], T.rC[:, :], True, l == 0)
-                if l > 0:
-                    m = PE.matmul(T.P0[:, 256 + c:512:4], T.Xh[:, :], T.rC[:, :], False, True)
+                m = PE.matmul(T.P3[:, c:256:4], T.X2[:, 128 * c:128 * c + 128], T.rC[:, :], True, True)
             return m
-        op("P", f, r=["X20", "X21", "Xh0", "Xh1", "rC"], w=["code"], b=["P0"])
+        op("P", f, r=["X20", "X21", "rC"], w=["code"], b=["P3"])
+        op("A", lambda: S.activation(T.nameT[:, :], T.P3[:, 0:256], AF.Copy), r=["code"], w=["nameT"], b=["P3"])
 
-    def select():
+    def q_to_psum(s):
+        pb = "P%d" % (6 + s // 2)
+        op("P", lambda: PE.matmul(T[pb][:, 256 * (s % 2):256 * (s % 2) + 256], T.eye[:, :], T.qa[:, blk(s)], True, True), r=["eye", "q%d" % s], w=["qP%d" % s], b=[pb])
+
+    def pieces(c, a, b):
+        return ["pr%d_%d" % (c, s) for s in range(a // TK, b // TK)]
+
+    def scores(l, c):
+        rs = T.rS[:, 0:8] if l == 0 else T.rS[:, 8:16]
+
+        def f():
+            for i in range(8):
+                m = PE.matmul(T.P0[:, 4 * i + c:256:32], T.prod[:, 1024 * c + i:1024 * (c + 1):8], rs, True, True)
+            return m
+        op("P", f, r=pieces(c, 0, 1024) + ["rS%d" % min(l, 1)], w=["S%d" % c], b=["P0"])
+
+    def keys(c, a, b):
+        return T.K[:, :].indirect(T.off[:, 64 * c + a // 16:64 * c + b // 16])
+
+    def gather_mul(c, a, b):
+        op("V", lambda: V.tensor_tensor(T.prod[:, 1024 * c + a:1024 * c + b], keys(c, a, b), T.qa[:, a:b], A.mult),
+           r=["K", "off"] + KB + QS[a // TK:b // TK], w=pieces(c, a, b))
+
+    def gather_raw(c, a, b):
+        op("A", lambda: S.activation(T.kraw[:, 1024 * c + a:1024 * c + b], keys(c, a, b), AF.Copy),
+           r=["K", "off"] + KB, w=["raw" + x for x in pieces(c, a, b)])
+
+    def raw_mul(c, a, b):
+        pb, o = "P%d" % (6 + a // 512), a % 512
+        op("V", lambda: V.tensor_tensor(T.prod[:, 1024 * c + a:1024 * c + b], T.kraw[:, 1024 * c + a:1024 * c + b], T[pb][:, o:o + b - a], A.mult),
+           r=["raw" + x for x in pieces(c, a, b)] + ["qP%d" % s for s in range(a // TK, b // TK)], w=pieces(c, a, b), b=[pb])
+
+    def select(l):
         ss = ["S%d" % c for c in range(C)]
+        fill = (lambda n: f_prod(l - 1, FILL[n])) if l > 0 else (lambda n: None)
+        fill(0)
         op("V", lambda: V.tensor_tensor_scan(T.run[:, :], T.rst[:, :], SC, 0.0, A.add, A.max), r=ss + ["rst"], w=["run"], b=["P0"])
+        fill(1)
         op("V", lambda: V.tensor_tensor(T.old[:, 1:256], T.P0[:, 1:256], T.run[:, 0:255], A.is_le), r=ss + ["run"], w=["old"], b=["P0"])
-        op("V", lambda: V.tensor_tensor_scan(T.win[:, :], T.old[:, :], CODE, 0.0, A.mult, A.max), r=["old", "old0", "code"], w=["win"], b=["P0"])
-        op("V", lambda: V.tensor_copy(T.ci[:, :, :], T.win[:, 3::4]), r=["win"], w=["ci"])
-        op("V", lambda: V.tensor_scalar(T.DI[:, 0::2, :], T.ci[:, :, :], 6, 63, SR, AND), r=["ci"], w=["DI0"])
-        op("V", lambda: V.tensor_scalar(T.DI[:, 1::2, :], T.ci[:, :, :], 63, None, AND), r=["ci"], w=["DI1"])
+        fill(2)
+        op("V", lambda: V.tensor_tensor_scan(T.win[:, :], T.old[:, :], T.nameT[:, :], 0.0, A.mult, A.max), r=["old", "old0", "nameT"], w=["win"])
+        fill(3)
+        if l == 0:
+            op("V", lambda: V.tensor_copy(T.ci[:, :, :], T.win[:, 3::4]), r=["win"], w=["ci"])
+        else:
+            op("V", lambda: V.tensor_tensor(T.ci[:, :, :], T.win[:, 3::4], hT, A.add), r=["win", "hT"], w=["ci"], b=["P0"])
+        op("V", lambda: V.tensor_scalar(T.DI[:, :, 0], T.ci[:, :, :], 6, 63, SR, AND), r=["ci"], w=["DI0"])
+        op("V", lambda: V.tensor_scalar(T.DI[:, :, 1], T.ci[:, :, :], 63, None, AND), r=["ci"], w=["DI1"])
         op("V", lambda: V.tensor_copy(T.DR[:, 0], T.DI[:, :, :]), r=["DI0", "DI1"], w=["D0"])
 
     def to_list():
-        for d in range(2):
-            for h in range(2):
-                op("A", lambda: S.activation(T.X[:, 8 * d:8 * d + 8, 8 * h:8 * h + 8], T.DR[:, 0, d::2, :], AF.Identity, scale=pmask[h]),
-                   r=["D0", "cG2", "cF"], w=["X%d%d" % (d, h)])
-            op("P", lambda: PE.matmul(LP, T.X[:, 8 * d:8 * d + 8, :], T.rL[:, 64 * d:64 * d + 64], d == 0, d == 1),
-               r=["X%d0" % d, "X%d1" % d, "rL0", "rL1"], w=["L"], b=["P2"])
-
-    def shifted():
-        for r_ in range(1, 4):
-            op("V", lambda: V.tensor_scalar(T.DR[:, r_], T.DR[:, 0], float(r_), None, A.subtract), r=["D0"], w=["D%d" % r_])
-
-    def shifted_far(n):
-        rows = slice(0, 16) if n == 4 else slice(2 * OC[1], 16)
-        op("A", lambda: S.activation(T.DR[:, n:2 * n, rows, :], T.DR[:, 0:n, rows, :], AF.Identity, bias=T.one[:, n // 4:n // 4 + 1]),
-           r=["D0", "D1", "D2", "D3", "one"] + (["D4"] if n == 8 else []), w=["D%d" % n])
-
-    def onehot(k, q0, q1):
-        for q in range(q0, q1):
-            v, n = RUNS[k][q]
-            op("V", lambda: V.tensor_scalar(T.OH[:, v:v + n, 2 * OC[k]:2 * OC[k + 1], :], T.DR[:, 0:n, 2 * OC[k]:2 * OC[k + 1], :],
-                                            float(v), None, A.is_equal), r=["D%d" % j for j in (0, 1, 2, 3, 4, 8) if j < n], w=["OH%d_%d" % (k, q)])
-
-    def counts(l, k):
-        HB = HBS[l]
+        for h in range(2):
+            op("A", lambda: S.activation(T.X[:, :, 16 * h:16 * h + 16], T.DR[:, 0], AF.Identity, scale=pmask[h]), r=["D0", "cG2", "cF"], w=["X%d" % h])
 
         def f():
-            for G in range(CH[k], CH[k + 1]):
-                j = (G - CH[k]) // 2 if l < RO - 1 else G // 2
-                o = T[HB[k]][64 * (G % 2):64 * (G % 2) + 64, 64 * j:64 * j + 64]
-                for i in range(8):
-                    m = PE.matmul(o, T.OH[:, :, 2 * G, i], T.OH[:, :, 2 * G + 1, i], i == 0, i == 7)
+            for d in range(2):
+                m = PE.matmul(LP, T.X[:, :, d::2], T.rL[:, 64 * d:64 * d + 64], d == 0, d == 1)
             return m
-        op("P", f, r=["OH%d_%d" % (k // 2, q) for q in range(len(RUNS[k // 2]))], w=["H%d" % k], b=[HB[k]])
+        op("P", f, r=["X0", "X1", "rL0", "rL1"], w=["L"], b=["P0"])
 
-    def new_bias(l, k):
-        HB = HBS[l]
-        cs = slice(32 * CH[k], 32 * CH[k + 1])
-        H = T[HB[k]][:, 0:32 * (CH[k + 1] - CH[k])]
-        op("V", lambda: V.tensor_scalar(H, H, 2.0, 1.0, A.min, A.subtract), r=["H%d" % k], w=["H%d" % k], b=[HB[k]])
-        op("V", lambda: V.tensor_tensor(T.bias[:, cs], T.bias[:, cs], H, A.subtract), r=["H%d" % k, "bias%d" % k], w=["bias%d" % k], b=[HB[k]])
+    def shifted(n):
+        op("V", lambda: V.tensor_scalar(T.DR[:, n:2 * n], T.DR[:, 0:n], float(n), None, A.subtract), r=["D0", "D1"][:n], w=["D%d" % n])
+
+    def shifted_far(e, j0, j1):
+        o, i = T.DR[:, 4:8, 32 * j0:32 * j1], T.DR[:, 0:4, 32 * j0:32 * j1]
+        fn = (lambda: V.tensor_scalar(o, i, 4.0, None, A.subtract)) if e == "V" else (lambda: S.activation(o, i, AF.Identity, bias=con(12)))
+        op(e, fn, r=["D0", "D1", "D2", "con12"], w=["D4_%d" % j for j in range(j0, j1)])
+
+    def tables(ch, q0, q1):
+        e, j0, j1, pb = ch
+        for q in range(q0, q1):
+            o, i = T.OH[:, REP * q:REP * q + REP, 32 * j0:32 * j1], T.DR[:, :, 32 * j0:32 * j1]
+            if e == "V":
+                fn = lambda: V.tensor_scalar(o, i, float(REP * q), None, A.is_equal)
+            else:
+                fn = lambda: S.activation(o, i, AF.Sign, bias=con(q))
+            op(e, fn, r=["D0", "D1", "D2", "con0"] + ["D4_%d" % j for j in range(j0, j1)], w=["OH%d_%d" % (j, q) for j in range(j0, j1)])
+
+    def counts(ch):
+        e, j0, j1, pb = ch
+
+        def f():
+            for G in range(2 * j0, 2 * j1):
+                ps, o = slice(64 * (G % 2), 64 * (G % 2) + 64), HC[pb] + 64 * (G // 2 - j0)
+                if e == "V":
+                    PE.matmul(T[pb][ps, o:o + 64], T.eye[:, ps], T.nb[:, 64 * (G // 2):64 * (G // 2) + 64], True, False)
+                for i in range(8):
+                    k = 16 * G + 2 * i
+                    if e == "V":
+                        m = PE.matmul(T[pb][ps, o:o + 64], T.OH[:, 0:64, k], T.OH[:, 0:64, k + 1], False, i == 7)
+                    else:
+                        m = PE.matmul(T.P5[ps, 128:193], T.OH[:, 0:64, k], T.OH[:, :, k + 1], i == 0, i == 7)
+            return m
+        op("P", f, r=["OH%d_%d" % (j, q) for j in range(j0, j1) for q in range(64 // REP)] + NB[j0:j1] + ["eye", "OHend"],
+           w=["H%d" % j for j in range(j0, j1)], b=[pb if e == "V" else "P5"])
+
+    def steps_out(ch):
+        op("A", lambda: S.activation(T.Ss[:, 0:65], T.P5[:, 128:193], AF.Copy), r=["H%d" % ch[1]], w=["Ss"], b=["P5"])
+
+    def differences(ch):
+        e, j0, j1, pb = ch
+        H = T[pb][:, HC[pb]:HC[pb] + 64]
+
+        def f():
+            PE.matmul(H, T.eye[:, :], T.nb[:, 64 * j0:64 * j1], True, False)
+            PE.matmul(H, T.Dp[:, :], T.Ss[:, 0:64], False, False)
+            return PE.matmul(H, T.Dn[:, :], T.Ss[:, 1:65], False, True)
+        op("P", f, r=["Ss", "Dp", "Dn", "eye", "nb%d" % j0], w=["H%d" % j0], b=[pb])
+
+    def new_bias(ch, k):
+        e, j0, j1, pb = ch
+        cs, js = slice(64 * j0, 64 * j1), range(j0, j1)
+        op("V", lambda: V.tensor_tensor(T.nb[:, cs], T[pb][:, HC[pb]:HC[pb] + 64 * (j1 - j0)], T.nb2[:, cs], A.min),
+           r=["H%d" % j for j in js] + ["nb2"], w=NB[j0:j1], b=[pb])
         rows = lambda a, b: T.K[16 * a + 15:16 * b + 16:16, :]
-        dmas("SSA"[k], "bias%d" % k, [(o, i) for i, o in bias_rows(T.bias, rows, k)], r=["bias%d" % k], w=["Kb%d" % k])
+        dmas("S", "bias%d" % k, [(o, i) for i, o in bias_rows(T.nb, rows, j0, j1)], r=NB[j0:j1], w=KB[j0:j1])
 
-    def last_bias():
-        H, hs = T.P0[:, 0:256], ["H0", "H1", "H2"]
-        op("V", lambda: V.tensor_scalar(H, H, 2.0, 1.0, A.min, A.subtract), r=hs, w=hs, b=["P0"])
-        op("V", lambda: V.tensor_tensor(T.biasF[:, :], T.bias[:, :], H, A.subtract), r=hs + ["bias0", "bias1", "bias2"], w=["biasF"], b=["P0"])
+    def last_bias(ch):
+        e, j0, j1, pb = ch
+        cs, js = slice(64 * j0, 64 * j1), range(j0, j1)
+        op("V", lambda: V.tensor_tensor(T.nbF[:, cs], T[pb][:, HC[pb]:HC[pb] + 64 * (j1 - j0)], T.nb2[:, cs], A.min),
+           r=["H%d" % j for j in js] + ["nb2"], w=["nbF%d" % j0], b=[pb])
+        op("A", lambda: S.activation(T.biasF[:, cs], T.nbF[:, cs], AF.Identity, bias=con(9), scale=-1.0), r=["nbF%d" % j0, "con9"], w=["bF%d" % j0])
         rows = lambda a, b: T.yb[a:b + 1, :]
-        dmas("S", "outb", [(o, i) for k in range(3) for i, o in bias_rows(T.biasF, rows, k)], r=["biasF"])
+        dmas("S", "outb", [(o, i) for i, o in bias_rows(T.biasF, rows, j0, j1)], r=["bF%d" % j0])
+
+    def bias_cap(l):
+        if l == 0:
+            op("A", lambda: S.activation(T.nb[:, :], T.bias[:, :], AF.Identity, scale=-1.0), r=["bias"], w=NB)
+            op("A", lambda: S.activation(T.nb2[:, :], T.bias[:, :], AF.Identity, bias=con(8), scale=-1.0), r=["bias", "con8"], w=["nb2"])
+        else:
+            op("A", lambda: S.activation(T.nb2[:, :], T.nb[:, :], AF.Identity, bias=con(8)), r=NB + ["con8"], w=["nb2"])
 
     def uv_out(l, p, u):
         o = (l * N + p) * 512 + 256 * u
         return (T.UVl if p == rank else T.UVs)[:, o:o + 256]
 
-    def gather_uv(q, l, p, u):
+    def gather_uv(l, p, u):
         src = (T.Uw, T.Vw)[u][:, :].indirect(T.woff[:, 16 * p:16 * p + 16])
-        fn = (lambda: V.tensor_copy(uv_out(l, p, u), src)) if q == "V" else (lambda: S.activation(uv_out(l, p, u), src, AF.Copy))
-        op(q, fn, r=["Uw", "Vw", "woff"], w=["uv%d_%d_%d" % (l, p, u)])
+        op("A", lambda: S.activation(uv_out(l, p, u), src, AF.Copy), r=["Uw", "Vw", "woff"], w=["uv%d_%d_%d" % (l, p, u)])
 
     def have(l, s, u):
-        return ["uv%d_%d_%d" % (l, s, u)] if s == rank else ["far%d_%d" % (l, s)]
+        return ["uv%d_%d_%d" % (l, s, u)] if s == rank else ["far%d_%d_%d" % (l, s, u)]
 
-    def shifts_a(l):
+    Wof = lambda l, s: T.Wl[:, 256 * l + 64 * s:256 * l + 64 * s + 64]
+
+    def winners_out(l):
+        op("V", lambda: V.tensor_scalar(Wof(l, rank), LP, 2048.0, None, A.subtract), r=["L"], w=["W%d_%d" % (l, rank)], b=["P0"])
+        to_all(Wof(l, rank), "arrW%d_" % l + "%d", ["W%d_%d" % (l, rank)], "W%d_" % l + "%d")
+
+    def winners_offsets():
+        op("V", lambda: V.tensor_copy(T.woff[:, :], LP), r=["L"], w=["woff"], b=["P0"])
+
+    def shift_sums(l):
+        op("P", lambda: PE.matmul(yP, T.eyeH[:, :], T.nmH[:, :], True, False), r=["eyeH", "nmH"], w=["y"], b=["P2"])
+        for s in srcs:
+            def f():
+                for c in range(C):
+                    m = PE.matmul(T.P2[:, 128 + 64 * c:192 + 64 * c], T.eyeH[:, :], Wof(l, s), False, s == srcs[-1] and c == C - 1)
+                return m
+            op("P", f, r=["W%d_%d" % (l, s)], w=["y"], b=["P2"])
+
         def f():
-            for s in range(N):
-                m = PE.matmul(hP, T.eyeF[:, :], T.Wl[:, 256 * l + 64 * s:256 * l + 64 * s + 64], s == 0, s == N - 1)
+            for n, s in enumerate(srcs):
+                m = PE.matmul(hP, T.eyeH[:, :], Wof(l, s), n == 0, n == N - 1)
             return m
-        op("P", f, r=["Wown%d" % l, "Wfar%d" % l, "eyeF"], w=["h"], b=["P0"])
+        op("P", f, r=["W%d_%d" % (l, s) for s in srcs], w=["h"], b=["P0"])
 
-    def shifts_b():
-        for c in range(C):
-            op("V", lambda: V.tensor_tensor(T.tI[:, 64 * c:64 * c + 64], T.nmI[:, 64 * c:64 * c + 64], hP, A.add),
-               r=["h", "nmI"], w=["tI%d" % c], b=["P0"])
+    def offsets(part):
+        if part == 0:
+            op("V", lambda: V.tensor_scalar(T.tI[:, :], yP, 5 * 2048.0, None, A.add), r=["y"], w=["tI"], b=["P2"])
+        elif part == 1:
+            op("V", lambda: V.tensor_scalar(T.tA[:, :], T.tI[:, :], E - 1, None, AND), r=["tI"], w=["tA"])
+        else:
+            op("V", lambda: V.tensor_copy(T.off[:, :], T.tA[:, :]), r=["tA"], w=["off"])
+
+    def shift_tokens():
         for h in range(2):
             op("A", lambda: S.activation(T.Xh[:, h::2], hP, AF.Identity, scale=hmask[h]), r=["h"], w=["Xh%d" % h], b=["P0"])
-        op("V", lambda: V.tensor_scalar(T.tA[:, :], T.tI[:, :], E - 1, None, AND), r=["tI%d" % c for c in range(C)], w=["tA"])
-        op("V", lambda: V.tensor_copy(T.off[:, :], T.tA[:, :]), r=["tA"], w=["off"])
+        op("P", lambda: PE.matmul(hT, T.Xh[:, :], T.rC[:, :], True, True), r=["Xh0", "Xh1", "rC"], w=["hT"], b=["P0"])
 
-    srcs = [rank] + peers[::-1]
-    dP, uP = T.P5[0:64, 0:256], T.P5[:, 256:512]
+    def f_prod(l, n):
+        s = srcs[n]
+        o = (l * N + s) * 512
+        op("V", lambda: V.tensor_tensor(T.Pf[:, blk(s)], T.UVl[:, o:o + 256], xP, A.mult), r=have(l, s, 0) + ["xP"], w=["Pf%d" % s], b=["P1"])
 
-    def f_prod(l, n0=0, n1=N):
-        for n in range(n0, n1):
+    def f_sum():
+        for n in FILL:
             s = srcs[n]
-            o = (l * N + s) * 512
-            op("V", lambda: V.tensor_tensor(T.Pf[:, 256 * s:256 * s + 256], T.UVl[:, o:o + 256], xP, A.mult), r=have(l, s, 0) + ["xP"], w=["Pf%d" % s], b=["P1"])
-            op("P", lambda: PE.matmul(dP, T.dsel[:, 64 * s:64 * s + 64], T.Pf[:, 256 * s:256 * s + 256], n == 0, n == N - 1),
-               r=["Pf%d" % s, "dsel"], w=["d"], b=["P5"])
+
+            def f():
+                for h in range(2):
+                    k = 4 * h + s
+                    m = PE.matmul(dP, T.dsel[:, 56 - 8 * k:184 - 8 * k], T.Pf[:, 256 * s + 128 * h:256 * s + 128 * h + 128],
+                                  n == FILL[0] and h == 0, n == FILL[-1] and h == 1)
+                return m
+            op("P", f, r=["Pf%d" % s, "dsel"], w=["d"], b=["P5"])
 
     def f_gate():
-        op("A", lambda: S.activation(T.tt[0:32, :], T.P5[0:32, 0:256], AF.Tanh, scale=2.0), r=["d"], w=["tt"], b=["P5"])
+        op("A", lambda: S.activation(T.tt[0:64, :], T.P5[0:64, 0:128], AF.Tanh, scale=2.0), r=["d"], w=["tt"], b=["P5"])
 
     def f_silu():
-        op("V", lambda: V.tensor_tensor(T.sS[0:64, :], T.tt[0:64, :], dP, A.mult), r=["tt", "tt1", "d"], w=["sS"], b=["P5"])
-        for n, s in enumerate(srcs):
-            pb = "P%d" % (3 + n // 2)
-            op("P", lambda: PE.matmul(T[pb][:, 256 * (n % 2):256 * (n % 2) + 256], T.bsel[0:64, 128 * s:128 * s + 128], T.sS[0:64, :], True, True),
-               r=["sS", "bsel%d" % s], w=["B%d" % s], b=[pb])
+        op("V", lambda: V.tensor_tensor(T.sS[:, :], T.tt[:, :], dP, A.mult), r=["tt", "tt1", "d"], w=["sS"], b=["P5"])
+
+    def f_spread(n):
+        s, pb = srcs[n], "P%d" % (3 + n % 2)
+
+        def f():
+            for h in range(2):
+                k, o = 4 * h + s, 256 * (n // 2) + 128 * h
+                m = PE.matmul(T[pb][:, o:o + 128], T.bsel[:, 128 * k:128 * k + 128], T.sS[:, :], True, True)
+            return m
+        op("P", f, r=["sS", "bsel%d" % s, "bsel%d" % (4 + s)], w=["B%d" % s], b=[pb])
 
     def mix(l, n):
         mm = T.mmF[:, 16:144] if l == RO - 1 else T.mmF[:, 0:128]
@@ -352,38 +458,40 @@ def rank_program(g, core, T, topo):
             op("P", lambda: PE.matmul(uP, mm, T.xS[:, :], True, False), r=["mmF0", "mmF1", "xS"], w=["u"], b=["P5"])
         else:
             s = srcs[n]
-            op("P", lambda: PE.matmul(uP, mm, T.Yf[:, 256 * s:256 * s + 256], False, n == N - 1), r=["Yf%d" % s], w=["u"], b=["P5"])
+            op("P", lambda: PE.matmul(uP, mm, T.Yf[:, blk(s)], False, n == N - 1), r=["Yf%d" % s], w=["u"], b=["P5"])
 
-    def f_y(l, n0, n1):
-        for n in range(n0, n1):
-            s = srcs[n]
-            pb = "P%d" % (3 + n // 2)
-            o = (l * N + s) * 512 + 256
-            op("V", lambda: V.tensor_tensor(T.Yf[:, 256 * s:256 * s + 256], T.UVl[:, o:o + 256], T[pb][:, 256 * (n % 2):256 * (n % 2) + 256], A.mult),
-               r=have(l, s, 1) + ["B%d" % s], w=["Yf%d" % s], b=[pb])
-            mix(l, n)
+    def f_y(l, n):
+        s, pb = srcs[n], "P%d" % (3 + n % 2)
+        o = (l * N + s) * 512 + 256
+        op("V", lambda: V.tensor_tensor(T.Yf[:, blk(s)], T.UVl[:, o:o + 256], T[pb][:, 256 * (n // 2):256 * (n // 2) + 256], A.mult),
+           r=have(l, s, 1) + ["B%d" % s], w=["Yf%d" % s], b=[pb])
 
     FB = ("P3", "P4", "P6", "P7")
 
-    def last_a(n):
-        s, pb, l = srcs[n], FB[n], RO - 1
-        o, cs = (l * N + s) * 512, slice(256 * s, 256 * s + 256)
-        op("V", lambda: V.tensor_tensor(T.Pf[:, cs], T.UVl[:, o:o + 256], xP, A.mult), r=have(l, s, 0) + ["xP"], w=["Pf%d" % s], b=["P1"])
-        op("P", lambda: PE.matmul(T[pb][:, 0:256], T.quart[:, :], T.Pf[:, cs], True, True), r=["Pf%d" % s, "quart"], w=["dl%d" % s], b=[pb])
-        op("A", lambda: S.activation(T.t4[:, cs], T[pb][:, 0:256], AF.Tanh, scale=2.0), r=["dl%d" % s], w=["t4%d" % s], b=[pb])
-        op("A", lambda: S.activation(T[pb][:, 256:512], T.t4[:, cs], AF.Identity, bias=T.one[:, 0:1]), r=["t4%d" % s, "one"], w=["t5%d" % s], b=[pb])
+    def last_sum(n):
+        s, pb = srcs[n], FB[n]
+        op("P", lambda: PE.matmul(T[pb][:, 0:256], T.quart[:, :], T.Pf[:, blk(s)], True, True), r=["Pf%d" % s, "quart"], w=["dl%d" % s], b=[pb])
 
-    def last_b(n):
-        s, pb, l = srcs[n], FB[n], RO - 1
-        o, cs = (l * N + s) * 512 + 256, slice(256 * s, 256 * s + 256)
-        op("V", lambda: V.tensor_tensor(T.Pf[:, cs], T.UVl[:, o:o + 256], T[pb][:, 0:256], A.mult), r=have(l, s, 1) + ["dl%d" % s], w=["Pf%d" % s], b=[pb])
-        op("V", lambda: V.tensor_tensor(T.Yf[:, cs], T.Pf[:, cs], T[pb][:, 256:512], A.mult), r=["Pf%d" % s, "t5%d" % s], w=["Yf%d" % s], b=[pb])
-        mix(l, n)
+    def last_gate(n):
+        s, pb = srcs[n], FB[n]
+        op("A", lambda: S.activation(T.t4[:, blk(s)], T[pb][:, 0:256], AF.Tanh, scale=2.0), r=["dl%d" % s], w=["t4%d" % s], b=[pb])
+        op("A", lambda: S.activation(T.Pf[:, blk(s)], T.t4[:, blk(s)], AF.Identity, bias=con(13)), r=["t4%d" % s, "con13"], w=["Pf%d" % s])
 
-    def f_tanh(l):
+    def last_silu(n):
+        s, pb = srcs[n], FB[n]
+        op("V", lambda: V.tensor_tensor(T[pb][:, 256:512], T.Pf[:, blk(s)], T[pb][:, 0:256], A.mult), r=["Pf%d" % s, "dl%d" % s], w=["t5%d" % s], b=[pb])
+
+    def last_y(n):
+        s, pb, l = srcs[n], FB[n], RO - 1
+        o = (l * N + s) * 512 + 256
+        op("V", lambda: V.tensor_tensor(T.Yf[:, blk(s)], T.UVl[:, o:o + 256], T[pb][:, 256:512], A.mult), r=have(l, s, 1) + ["t5%d" % s], w=["Yf%d" % s], b=[pb])
+
+    def f_tanh(l, parts=(0, 1)):
         if l < RO - 1:
-            op("A", lambda: S.activation(xP, uP, AF.Tanh, scale=0.5), r=["u"], w=["xP"], b=["P5", "P1"])
-            op("A", lambda: S.activation(T.xS[:, :], uP, AF.Tanh, scale=0.5), r=["u"], w=["xS"], b=["P5"])
+            if 0 in parts:
+                op("A", lambda: S.activation(xP, uP, AF.Tanh, scale=0.5), r=["u"], w=["xP"], b=["P5", "P1"])
+            if 1 in parts:
+                op("A", lambda: S.activation(T.xS[:, :], uP, AF.Tanh, scale=0.5), r=["u"], w=["xS"], b=["P5"])
         else:
             op("A", lambda: S.activation(T.xo[:, :], uP, AF.Tanh, scale=0.5), r=["u"], w=["xo"], b=["P5"])
             dmas("A", "outx", [(T.yx[:, :], T.xo[:, :])], r=["xo"])
@@ -394,131 +502,163 @@ def rank_program(g, core, T, topo):
         op("A", lambda: S.activation(T.mmF[:, 16:144], T.mmB[:, :], AF.Copy), r=["mmB"], w=["mmF0"])
         op("A", lambda: S.activation(T.mmF[:, 0:16], T.mmB[:, 112:128], AF.Copy), r=["mmB"], w=["mmF1"])
 
+    names()
     for l in range(RO):
-        last = l == RO - 1
+        last, x = l == RO - 1, l - 1
         if l == 0:
-            names()
-            names_pe(0)
-            a, b = rank * TK, (rank + 1) * TK
-            far = [(x if x != a else b, x + 512 if x + 512 != b else a) for x in (0, 512)]
-            for c in (3, 2, 1):
-                gather_raw(c, far)
+            for s in srcs[1:]:
+                for c in (3, 2, 1):
+                    gather_raw(c, s * TK, s * TK + TK)
+            count_constants(0)
             for c in range(C):
-                gather_mul(c, a, b, "prodc", ["qown"])
-            later_constants(0)
-            q_to_psum()
-            gather_mul(0, far[0][0], far[0][1], "prod", ["qfar"])
-            gather_mul(0, far[1][0], far[1][1], "prodb", ["qfar"])
-            scores(0)
-            for c in (3, 2, 1):
-                raw_mul(c, far)
-                scores(c)
-        elif l == 1:
-            gather_raw(3)
-            gather_raw(2)
-            x_start()
-            for c in range(2):
-                gather_mul(c, 0, 1024, "prod", ["qown", "qfar"])
-                if c == 0:
-                    names_pe(l)
-                scores(c)
-            for c in (3, 2):
-                raw_mul(c)
-                scores(c)
+                gather_mul(c, rank * TK, rank * TK + TK)
+            count_constants(1)
+            for s in srcs[1:]:
+                q_to_psum(s)
+                gather_mul(0, s * TK, s * TK + TK)
+                if s == srcs[-1]:
+                    scores(l, 0)
+                for c in (3, 2, 1):
+                    raw_mul(c, s * TK, s * TK + TK)
+                    if s == srcs[-1]:
+                        scores(l, c)
+            q_to_psum(rank)
+            bias_cap(l)
         else:
-            gather_raw(3)
-            f_gate()
-            gather_raw(2)
-            gather_raw(1)
-            gather_mul(0, 0, 1024, "prod", ["qown", "qfar"])
-            names_pe(l)
-            scores(0)
-            mix(l - 2, -1)
-            raw_mul(3)
-            scores(3)
-            f_silu()
-            raw_mul(2)
-            scores(2)
-            f_y(l - 2, 0, 2)
-            raw_mul(1)
-            scores(1)
-            f_y(l - 2, 2, 4)
-            f_tanh(l - 2)
-        select()
+            for part in RAW:
+                gather_raw(*part)
+            gather_mul(0, 0, 1024)
+            scores(l, 0)
+            gather_mul(1, 0, 256)
+            for k, part in enumerate(RAW):
+                raw_mul(*part)
+                if k % 2:
+                    scores(l, part[0])
+            if l > 1:
+                f_tanh(l - 2, (0,))
+            gather_uv(x, rank, 0)
+            if l > 1:
+                f_tanh(l - 2, (1,))
+            gather_uv(x, rank, 1)
+            bias_cap(l)
+        select(l)
+        if l > 0:
+            f_sum()
+        if last:
+            mix(x, -1)
         to_list()
+        shifted(1)
+        shifted(2)
+        if l > 0:
+            f_gate()
         if not last:
-            wo = T.Wl[:, 256 * l + 64 * rank:256 * l + 64 * rank + 64]
-            shifted()
-            shifted_far(4)
-            op("A", lambda: S.activation(wo, LP, AF.Copy), r=["L"], w=["Wown%d" % l], b=["P2"])
-            to_all(wo, "arrW%d" % l, ["Wown%d" % l])
-            arrives("arrW%d" % l, 3 * len(eng), "Wfar%d" % l)
-            shifted_far(8)
-            onehot(0, 0, 5)
-            op("V", lambda: V.tensor_copy(T.woff[:, :], wo), r=["Wown%d" % l], w=["woff"])
-            for p in peers + [rank]:
-                gather_uv("A", l, p, 0)
-                gather_uv("A", l, p, 1)
-            onehot(0, 5, len(RUNS[0]))
-            counts(l, 0)
-            counts(l, 1)
-            onehot(1, 0, 3)
-            new_bias(l, 0)
-            onehot(1, 3, 4)
-            counts(l, 2)
-            shifts_a(l)
-            new_bias(l, 1)
+            c0, c1, c2, ca = MID
+            shifted_far(*ca[:3])
+            shifted_far("V", c0[1], c2[2])
+            tables(ca, 0, 8)
+            tables(c0, 0, 2)
+            winners_out(l)
             if l > 0:
-                f_prod(l - 1, 0, 1)
-            new_bias(l, 2)
+                f_silu()
+                f_spread(0)
+            tables(c0, 2, 8)
+            counts(c0)
             if l > 0:
-                f_prod(l - 1, 1, 2)
-            shifts_b()
+                f_spread(1)
+            winners_offsets()
+            tables(c1, 0, 5)
+            new_bias(c0, 0)
+            tables(c1, 5, 8)
+            counts(ca)
+            counts(c1)
+            if l == 0:
+                steps_out(ca)
+            for u in range(2):
+                gather_uv(l, peers[0], u)
             if l > 0:
-                f_prod(l - 1, 2, 4)
+                steps_out(ca)
+            to_home(l, [(0, 0, 2)])
+            tables(c2, 0, 5)
+            new_bias(c1, 1)
+            differences(ca)
+            tables(c2, 5, 8)
+            counts(c2)
+            new_bias(ca, 2)
+            if l > 0:
+                f_y(x, 0)
+            new_bias(c2, 3)
+            if l > 0:
+                f_y(x, 1)
             else:
-                later_constants(1)
-            for k in range(N - 1):
-                to_home(l, k, KB)
+                x_constants(0)
+                x_constants(1)
+            for u in range(2):
+                gather_uv(l, peers[1], u)
+            shift_sums(l)
+            for u in range(2):
+                gather_uv(l, peers[2], u)
+            if l > 0:
+                f_spread(2)
+                f_spread(3)
+            offsets(0)
+            offsets(1)
+            if l > 0:
+                f_y(x, 2)
+            offsets(2)
+            shift_tokens()
+            if l > 0:
+                f_y(x, 3)
+                for n in range(-1, N):
+                    mix(x, n)
+            else:
+                x_constants(2)
+                x_start()
+            for k in range(1, N - 1):
+                to_home(l, [(k, 0, 2)], KB)
         else:
-            f_prod(l - 1, 0, 1)
-            shifted()
-            shifted_far(4)
-            f_prod(l - 1, 1, 3)
-            op("V", lambda: V.tensor_copy(T.woff[:, :], LP), r=["L"], w=["woff"], b=["P2"])
-            f_prod(l - 1, 3, 4)
-            mix(l - 1, -1)
-            for k, p in enumerate(peers):
-                gather_uv("V" if k == 0 else "A", l, p, 0)
-                gather_uv("A", l, p, 1)
-                to_home(l, k, [])
-                if k == 1:
-                    f_gate()
-            shifted_far(8)
-            gather_uv("A", l, rank, 0)
-            gather_uv("A", l, rank, 1)
-            onehot(0, 0, 5)
+            c0, c1 = END
+            shifted_far("V", 0, 4)
+            winners_offsets()
+            for u in range(2):
+                for p in peers:
+                    gather_uv(l, p, u)
+            to_home(l, [(0, 0, 1), (1, 0, 1)])
+            to_home(l, [(2, 0, 1), (0, 1, 2)])
+            to_home(l, [(1, 1, 2), (2, 1, 2)])
             f_silu()
-            onehot(0, 5, 7)
-            f_y(l - 1, 0, 2)
-            onehot(0, 7, 8)
-            f_y(l - 1, 2, 4)
-            f_tanh(l - 1)
-            onehot(0, 8, 10)
-            counts(l, 0)
-            onehot(1, 0, 4)
-            last_a(0)
-            last_a(1)
-            last_a(2)
-            last_a(3)
-            counts(l, 1)
-            counts(l, 2)
-            mix(l, -1)
-            last_b(0)
-            last_b(1)
-            last_b(2)
-            last_bias()
-            last_b(3)
+            f_spread(0)
+            f_spread(1)
+            tables(c0, 0, 2)
+            for n in range(N):
+                f_y(x, n)
+                if n < 2:
+                    f_spread(n + 2)
+                tables(c0, n + 2, n + 3)
+                mix(x, n)
+            gather_uv(l, rank, 0)
+            gather_uv(l, rank, 1)
+            f_tanh(x)
+            tables(c0, 6, 8)
+            counts(c0)
+            tables(c1, 0, 1)
+            for n in range(N):
+                f_prod(l, n)
+                last_sum(n)
+                last_gate(n)
+                tables(c1, 1 + 2 * n, min(3 + 2 * n, 8))
+                if n == 1:
+                    mix(l, -1)
+                if n > 0:
+                    last_silu(n - 1)
+            counts(c1)
+            last_bias(c0)
+            last_y(0)
+            last_silu(3)
+            for n in range(N):
+                if n > 0:
+                    last_y(n)
+                mix(l, n)
+            last_bias(c1)
             f_tanh(l)
     for s in total:
         if max(seen[q].get(s, 0) for q in Q) < total[s]:

@@ -4,21 +4,23 @@ from concourse.mybir import AluOpType, ActivationFunctionType
 N, E, TK, C, RO = 4, 4096, 256, 4, 4
 REP = 8
 F32, BF, I32, U16, F16 = "float32", "bfloat16", "int32", "uint16", "float16"
-MID = [("V", 0, 1, "P1"), ("V", 1, 2, "P2"), ("V", 2, 3, "P1"), ("A", 3, 4, "P0")]
-END = [("V", 0, 2, "P0"), ("V", 2, 4, "P2")]
-HC = {"P0": 384, "P1": 0, "P2": 0}
-FILL = (1, 2, 0, 3)
-RAW = [(3, 0, 512), (3, 512, 1024), (2, 0, 512), (2, 512, 1024), (1, 512, 1024), (1, 256, 512)]
+MID = [("V", 0, 1, "P1"), ("V", 1, 2, "P2"), ("V", 2, 3, "P3"), ("A", 3, 4, "P4")]
+END = [("V", 0, 2, "P0"), ("V", 2, 4, "P1")]
+HC = {"P0": 384, "P1": 0, "P2": 0, "P3": 256, "P4": 256}
+FILL = (0, 1, 2, 3)
+RAW = [(3, 0, 1024), (2, 0, 1024), (1, 512, 1024)]
+SENDS = ([(0, 0), (1, 0)], [(2, 0)], [(0, 1), (1, 1)], [(2, 1)])
+FIRST = [(0, 0), (0, 1), (0, 2), (0, 3), (1, 0), (1, 3), (2, 0), (2, 3), (1, 2), (2, 2), (3, 0), (3, 3), (3, 2), (1, 1), (2, 1), (3, 1)]
 
 SCRATCH = {
     "K": ("sbuf", [128, E], BF), "Uw": ("sbuf", [128, E], BF), "Vw": ("sbuf", [128, E], BF),
-    "nmI": ("sbuf", [128, 256], I32), "nmC": ("sbuf", [128, 256], F32), "nmH": ("sbuf", [128, 256], F16), "qa": ("sbuf", [128, 1024], BF),
+    "nmI": ("sbuf", [128, 256], I32), "nmC": ("sbuf", [128, 256], F32), "nmH": ("sbuf", [128, 256], F32), "qa": ("sbuf", [128, 1024], BF),
     "off": ("sbuf", [128, 256], U16), "woff": ("sbuf", [128, 64], U16), "tI": ("sbuf", [128, 256], I32), "tA": ("sbuf", [128, 256], I32),
     "prod": ("sbuf", [128, 4096], F16), "kraw": ("sbuf", [128, 4096], BF),
-    "Xh": ("sbuf", [128, 128], F32), "X2": ("sbuf", [128, 512], F32), "nameT": ("sbuf", [128, 256], F32),
+    "Xh": ("sbuf", [128, 128], F32), "X2": ("sbuf", [128, 512], F32),
     "run": ("sbuf", [128, 256], F32), "old": ("sbuf", [128, 256], F32), "win": ("sbuf", [128, 256], F32),
     "rst": ("sbuf", [128, 256], F32), "ci": ("sbuf", [128, 8, 8], I32), "DI": ("sbuf", [128, 64, 2], I32),
-    "DR": ("sbuf", [128, REP, 128], BF), "X": ("sbuf", [128, 8, 32], BF), "OH": ("sbuf", [128, 65, 128], BF),
+    "DR": ("sbuf", [128, 2 * REP, 128], BF), "X": ("sbuf", [128, 8, 32], BF), "OH": ("sbuf", [128, 65, 128], BF),
     "bias": ("sbuf", [128, 256], BF), "nb": ("sbuf", [128, 256], BF), "nb2": ("sbuf", [128, 256], BF),
     "nbF": ("sbuf", [128, 256], F32), "biasF": ("sbuf", [128, 256], F32), "Ss": ("sbuf", [128, 128], F32),
     "Wl": ("sbuf", [128, 3 * 256], F16), "UVs": ("sbuf", [128, RO * N * 512], BF), "UVl": ("sbuf", [128, RO * N * 512], BF),
@@ -29,9 +31,9 @@ SCRATCH = {
     "Jn": ("sbuf", [128, 128], F32), "Jd": ("sbuf", [128, 192], F32), "Jb": ("sbuf", [128, 128], F32),
     "rS": ("sbuf", [128, 16], F16), "rC": ("sbuf", [128, 64], F32), "rL": ("sbuf", [128, 128], BF),
     "eye": ("sbuf", [128, 128], BF), "eyeH": ("sbuf", [128, 128], F16),
-    "Da": ("sbuf", [128, 128], F32), "Db": ("sbuf", [128, 128], F32), "Dp": ("sbuf", [128, 128], F32), "Dn": ("sbuf", [128, 128], F32),
+    "Dp": ("sbuf", [128, 128], F32), "Dn": ("sbuf", [128, 128], F32),
     "quart": ("sbuf", [128, 128], F32), "t4": ("sbuf", [128, 1024], F32),
-    "con": ("sbuf", [128, 16], F32), "dsel": ("sbuf", [128, 192], F32), "bsel": ("sbuf", [128, 1024], F32),
+    "dist": ("sbuf", [128, 256], BF), "con": ("sbuf", [128, 16], F32), "dsel": ("sbuf", [128, 192], F32), "bsel": ("sbuf", [128, 1024], F32),
 }
 for _b in range(8):
     SCRATCH["P%d" % _b] = ("psum", [128, 512], F32)
@@ -116,24 +118,25 @@ def rank_program(g, core, T, topo):
         for p in peers:
             arrives(sem % p, len(eng), name % p)
 
-    def to_home(l, parts, more=()):
-        es = [eng[j::len(parts)] for j in range(len(parts))]
-        trs = []
-        for (k, u0, u1), e in zip(parts, es):
-            p, s = peers[k], (rank - k - 1) % N
-            order("G", ["uv%d_%d_%d" % (l, p, u) for u in range(u0, u1)] + list(more), (), (), True)
-            so, do = (l * N + p) * 512, (l * N + rank) * 512
-            trs.append(RemoteDMATransfer(dst_ids=[dst(p)], dma_engine_mask=bits(e), remote_sem=T.sem["arrU%d_%d_%d" % (l, rank, u0)],
-                                         src=T.UVs[:, so + 256 * u0:so + 256 * u1], dst=T.UVl[:, do + 256 * u0:do + 256 * u1]))
-            total["sent"] = total.get("sent", 0) + len(e)
-            arrives("arrU%d_%d_%d" % (l, s, u0), len(e), "far%d_%d_%d" % (l, s, u0))
-            for u in range(u0 + 1, u1):
-                lastw["far%d_%d_%d" % (l, s, u)] = lastw["far%d_%d_%d" % (l, s, u0)]
-        g.remote_dma_fused(trs, local_sem=T.sem.sent)
+    def place(l, s, u):
+        o = ((2 * l + u) * N + s) * TK
+        return slice(o, o + TK)
+
+    def send_uv(l, calls, more=()):
+        for parts in calls:
+            trs = []
+            for j, (k, u) in enumerate(parts):
+                p, s, e = peers[k], (rank - k - 1) % N, eng[j::len(parts)]
+                order("G", ["uv%d_%d_%d" % (l, u, p)] + list(more), (), (), True)
+                trs.append(RemoteDMATransfer(dst_ids=[dst(p)], dma_engine_mask=bits(e), remote_sem=T.sem["arrU%d_%d_%d" % (l, rank, u)],
+                                             src=T.UVs[:, place(l, p, u)], dst=T.UVl[:, place(l, rank, u)]))
+                total["sent"] = total.get("sent", 0) + len(e)
+                arrives("arrU%d_%d_%d" % (l, s, u), len(e), "far%d_%d_%d" % (l, s, u))
+            g.remote_dma_fused(trs, local_sem=T.sem.sent)
 
     V, S, PE = g.vector, g.scalar, g.tensor
-    SC, hT, LP, hP = T.P0[:, 0:256], T.P0[:, 256:320], T.P0[:, 320:384], T.P0[:, 0:64]
-    xP, yP = T.P1[:, 256:512], T.P2[:, 128:384]
+    SC, NM, hT, LP, hP = T.P0[:, 0:256], T.P0[:, 256:512], T.P2[:, 384:448], T.P2[:, 448:512], T.P0[:, 0:64]
+    xP = T.P1[:, 256:512]
     dP, uP = T.P5[:, 0:128], T.P5[:, 256:512]
     KB, NB, QS = ["Kb%d" % j for j in range(4)], ["nb%d" % j for j in range(4)], ["q%d" % s for s in range(N)]
 
@@ -166,11 +169,11 @@ def rank_program(g, core, T, topo):
     cf = lambda j: T.cF[:, j:j + 1]
     cg = lambda j: T.cG[:, j:j + 1]
     con = lambda j: T.con[:, j:j + 1]
-    for j, v in ((10, 20.0), (8, 2.0), (9, 4.0), (12, -4.0), (13, 1.0)):
+    for j, v in ((10, 20.0), (8, 2.0), (9, 4.0), (13, 1.0), (14, -56.0)):
         op("V", lambda: V.memset(con(j), v), w=["con%d" % j])
     op("A", lambda: S.activation(T.tt[64:128, :], T.Jn[64:128, :], AF.Tanh, bias=T.con[64:128, 10:11]), r=["Jn", "con10"], w=["tt1"])
-    cols = [(p0, 4, 7), (p0, 0, 63), (p0, 0, 7), (p16, 4, 7), (p0, 3, 1), (p0, 0, 1), (p0, 1, 63), (p0, 0, 127), (p0, 0, 15)]
-    for j, (src, sh, m) in enumerate(cols):
+    cuts = [(p0, 4, 7), (p0, 0, 63), (p0, 0, 7), (p16, 4, 7), (p0, 3, 1), (p0, 0, 1), (p0, 1, 63), (p0, 0, 127), (p0, 0, 15)]
+    for j, (src, sh, m) in enumerate(cuts):
         op("V", lambda: V.tensor_scalar(T.cI[:, j:j + 1], src, sh, m, SR, AND), r=["pI"], w=["cI%d" % j])
     op("V", lambda: V.tensor_copy(T.cF[:, 0:9], T.cI[:, 0:9]), r=["cI%d" % j for j in range(9)], w=["cF"])
     op("V", lambda: V.memset(T.old[:, 0:1], 0.0), w=["old0"])
@@ -190,25 +193,16 @@ def rank_program(g, core, T, topo):
     op("V", lambda: V.tensor_scalar(T.rL[:, 64:128], T.Jn[:, 0:64], cf(6), None, A.is_equal), r=["cF", "Jn"], w=["rL1"])
     op("V", lambda: V.tensor_scalar(T.con[:, 0:8], T.Jn[:, 0:8], -float(REP), 0.5, A.mult, A.add), r=["Jn"], w=["con0"])
 
-    def count_constants(part):
-        if part == 1:
-            op("V", lambda: V.tensor_scalar(T.nmH[:, :], T.nmI[:, :], 2048.0, None, A.subtract), r=["nmI"], w=["nmH"])
-            op("V", lambda: V.tensor_scalar(T.eyeH[:, :], T.eye[:, :], 1.0, None, A.mult), r=["eye"], w=["eyeH"])
-            op("V", lambda: V.memset(T.OH[:, 64], -1.0), w=["OHend"])
-            op("V", lambda: V.tensor_scalar(T.rS[:, 8:16], T.Jn[:, 0:8], cf(3), cg(7), A.is_equal, A.mult), r=["cF", "Jn", "cG7"], w=["rS1"])
-            return
-        op("V", lambda: V.tensor_scalar(cg(4), cf(1), 0.0, 0.25, A.is_equal, A.mult), r=["cF"], w=["cG4"])
-        op("V", lambda: V.tensor_scalar(cg(5), cf(1), 0.0, -0.25, A.not_equal, A.mult), r=["cF"], w=["cG5"])
-        op("V", lambda: V.tensor_scalar(cg(8), cf(7), 1.0, None, A.subtract), r=["cF"], w=["cG8"])
-        op("V", lambda: V.tensor_scalar(cg(9), cf(7), 63.0, None, A.add), r=["cF"], w=["cG9"])
-        op("V", lambda: V.tensor_scalar(cg(6), cf(8), 15.0, -2.0, A.is_equal, A.mult), r=["cF"], w=["cG6"])
-        op("V", lambda: V.tensor_scalar(T.Da[:, :], T.Jn[:, :], cg(8), cg(5), A.is_equal, A.mult), r=["Jn", "cG8", "cG5"], w=["Da"])
-        op("V", lambda: V.tensor_scalar(T.Db[:, :], T.Jn[:, :], cg(9), cg(4), A.is_equal, A.mult), r=["Jn", "cG9", "cG4"], w=["Db"])
-        op("V", lambda: V.tensor_scalar(T.Dn[:, :], T.Jn[:, :], cf(7), 0.25, A.is_equal, A.mult), r=["Jn", "cF"], w=["Dq"])
-        op("V", lambda: V.tensor_scalar(cg(7), cg(6), 1.0, None, A.add), r=["cG6"], w=["cG7"])
-        op("V", lambda: V.tensor_tensor(T.Da[:, :], T.Da[:, :], T.Db[:, :], A.add), r=["Da", "Db"], w=["Da"])
-        op("V", lambda: V.tensor_tensor(T.Dp[:, :], T.Da[:, :], T.Dn[:, :], A.add), r=["Da", "Dq"], w=["Dp"])
-        op("V", lambda: V.tensor_scalar(T.Dn[:, :], T.Dp[:, :], -1.0, None, A.mult), r=["Dp"], w=["Dn"])
+    op("V", lambda: V.tensor_scalar(cg(6), cf(8), 15.0, -2.0, A.is_equal, A.mult), r=["cF"], w=["cG6"])
+    op("V", lambda: V.tensor_scalar(T.nmH[:, :], T.nmI[:, :], 4 * 2048.0, None, A.add), r=["nmI"], w=["nmH"])
+    op("V", lambda: V.tensor_scalar(cg(7), cg(6), 1.0, None, A.add), r=["cG6"], w=["cG7"])
+    op("V", lambda: V.tensor_scalar(T.eyeH[:, :], T.eye[:, :], 1.0, None, A.mult), r=["eye"], w=["eyeH"])
+    op("V", lambda: V.memset(T.OH[:, 64], -1.0), w=["OHend"])
+    op("V", lambda: V.tensor_scalar(T.rS[:, 8:16], T.Jn[:, 0:8], cf(3), cg(7), A.is_equal, A.mult), r=["cF", "Jn", "cG7"], w=["rS1"])
+    for D, name, v in ((T.Dp, "Dp", 0.25), (T.Dn, "Dn", -0.25)):
+        op("G", lambda: g.iota(D[:, :], [[0, 128]], 0, 0, **flt), w=[name])
+        for fill, step, base, cm in ((v, -1, 0, 1), (-v, -1, -1, 1), (0.0, 1, -64 * 128 - 63, 128), (v, 1, -63, 128), (v, 1, -64 * 128 - 127, 128)):
+            op("G", lambda: g.affine_select(D[:, :], D[:, :], [[step, 128]], A.not_equal, fill, base, cm), r=[name], w=[name])
 
     def x_constants(part):
         if part == 0:
@@ -219,8 +213,8 @@ def rank_program(g, core, T, topo):
         for k in range(4 * part - 4, 4 * part):
             op("V", lambda: V.tensor_scalar(T.bsel[:, 128 * k:128 * k + 128], T.Jb[:, :], float(8 * k), cf(1), A.add, A.is_equal), r=["Jb", "cF"], w=["bsel%d" % k])
 
-    dmas("S", "ldb", bias_rows(T.bias, kerows, 0, 4), r=["qleft"], w=["bias"])
-    dmas("S", "lduv", turned(T.Uw, T.ue) + turned(T.Vw, T.ve), w=["Uw", "Vw"])
+    dmas("S", "ldb", bias_rows(T.bias, kerows, 0, 4), r=["K"], w=["bias"])
+    dmas("S", "lduv", turned(T.Uw, T.ue) + turned(T.Vw, T.ve), r=["qleft"], w=["Uw", "Vw"])
     dmas("S", "ldx", turned(T.xB, T.x0) + turned(T.mmB, T.mm), w=["xB", "mmB"])
 
     hmask = (cg(2), cf(4))
@@ -233,10 +227,9 @@ def rank_program(g, core, T, topo):
 
         def f():
             for c in range(C):
-                m = PE.matmul(T.P3[:, c:256:4], T.X2[:, 128 * c:128 * c + 128], T.rC[:, :], True, True)
+                m = PE.matmul(T.P0[:, 256 + c:512:4], T.X2[:, 128 * c:128 * c + 128], T.rC[:, :], True, True)
             return m
-        op("P", f, r=["X20", "X21", "rC"], w=["code"], b=["P3"])
-        op("A", lambda: S.activation(T.nameT[:, :], T.P3[:, 0:256], AF.Copy), r=["code"], w=["nameT"], b=["P3"])
+        op("P", f, r=["X20", "X21", "rC"], w=["names"], b=["P0"])
 
     def q_to_psum(s):
         pb = "P%d" % (6 + s // 2)
@@ -245,14 +238,14 @@ def rank_program(g, core, T, topo):
     def pieces(c, a, b):
         return ["pr%d_%d" % (c, s) for s in range(a // TK, b // TK)]
 
-    def scores(l, c):
+    def scores(l, c, a=0, b=1024):
         rs = T.rS[:, 0:8] if l == 0 else T.rS[:, 8:16]
 
         def f():
             for i in range(8):
-                m = PE.matmul(T.P0[:, 4 * i + c:256:32], T.prod[:, 1024 * c + i:1024 * (c + 1):8], rs, True, True)
+                m = PE.matmul(T.P0[a // 8:b // 8, 4 * i + c:256:32], T.prod[:, 1024 * c + a + i:1024 * c + b:8], rs, True, True)
             return m
-        op("P", f, r=pieces(c, 0, 1024) + ["rS%d" % min(l, 1)], w=["S%d" % c], b=["P0"])
+        op("P", f, r=pieces(c, a, b) + ["rS%d" % min(l, 1)], w=["S" + x for x in pieces(c, a, b)], b=["P0"])
 
     def keys(c, a, b):
         return T.K[:, :].indirect(T.off[:, 64 * c + a // 16:64 * c + b // 16])
@@ -271,19 +264,18 @@ def rank_program(g, core, T, topo):
            r=["raw" + x for x in pieces(c, a, b)] + ["qP%d" % s for s in range(a // TK, b // TK)], w=pieces(c, a, b), b=[pb])
 
     def select(l):
-        ss = ["S%d" % c for c in range(C)]
+        ss = ["S" + x for c in range(C) for x in pieces(c, 0, 1024)]
         fill = (lambda n: f_prod(l - 1, FILL[n])) if l > 0 else (lambda n: None)
         fill(0)
         op("V", lambda: V.tensor_tensor_scan(T.run[:, :], T.rst[:, :], SC, 0.0, A.add, A.max), r=ss + ["rst"], w=["run"], b=["P0"])
         fill(1)
         op("V", lambda: V.tensor_tensor(T.old[:, 1:256], T.P0[:, 1:256], T.run[:, 0:255], A.is_le), r=ss + ["run"], w=["old"], b=["P0"])
         fill(2)
-        op("V", lambda: V.tensor_tensor_scan(T.win[:, :], T.old[:, :], T.nameT[:, :], 0.0, A.mult, A.max), r=["old", "old0", "nameT"], w=["win"])
-        fill(3)
+        op("V", lambda: V.tensor_tensor_scan(T.win[:, :], T.old[:, :], NM, 0.0, A.mult, A.max), r=["old", "old0", "names"], w=["win"], b=["P0"])
         if l == 0:
             op("V", lambda: V.tensor_copy(T.ci[:, :, :], T.win[:, 3::4]), r=["win"], w=["ci"])
         else:
-            op("V", lambda: V.tensor_tensor(T.ci[:, :, :], T.win[:, 3::4], hT, A.add), r=["win", "hT"], w=["ci"], b=["P0"])
+            op("V", lambda: V.tensor_tensor(T.ci[:, :, :], T.win[:, 3::4], hT, A.add), r=["win", "hT"], w=["ci"], b=["P2"])
         op("V", lambda: V.tensor_scalar(T.DI[:, :, 0], T.ci[:, :, :], 6, 63, SR, AND), r=["ci"], w=["DI0"])
         op("V", lambda: V.tensor_scalar(T.DI[:, :, 1], T.ci[:, :, :], 63, None, AND), r=["ci"], w=["DI1"])
         op("V", lambda: V.tensor_copy(T.DR[:, 0], T.DI[:, :, :]), r=["DI0", "DI1"], w=["D0"])
@@ -296,25 +288,30 @@ def rank_program(g, core, T, topo):
             for d in range(2):
                 m = PE.matmul(LP, T.X[:, :, d::2], T.rL[:, 64 * d:64 * d + 64], d == 0, d == 1)
             return m
-        op("P", f, r=["X0", "X1", "rL0", "rL1"], w=["L"], b=["P0"])
+        op("P", f, r=["X0", "X1", "rL0", "rL1"], w=["L"], b=["P2"])
 
     def shifted(n):
         op("V", lambda: V.tensor_scalar(T.DR[:, n:2 * n], T.DR[:, 0:n], float(n), None, A.subtract), r=["D0", "D1"][:n], w=["D%d" % n])
 
-    def shifted_far(e, j0, j1):
-        o, i = T.DR[:, 4:8, 32 * j0:32 * j1], T.DR[:, 0:4, 32 * j0:32 * j1]
-        fn = (lambda: V.tensor_scalar(o, i, 4.0, None, A.subtract)) if e == "V" else (lambda: S.activation(o, i, AF.Identity, bias=con(12)))
-        op(e, fn, r=["D0", "D1", "D2", "con12"], w=["D4_%d" % j for j in range(j0, j1)])
+    def shifted_far(n):
+        cs = slice(0, 128) if n == 4 else slice(96, 128)
+        op("V", lambda: V.tensor_scalar(T.DR[:, n:2 * n, cs], T.DR[:, 0:n, cs], float(n), None, A.subtract), r=["D0", "D1", "D2", "D4"][:2 + n // 4], w=["D%d" % n])
 
-    def tables(ch, q0, q1):
+    def tables(ch, q0, q1, n=1):
         e, j0, j1, pb = ch
-        for q in range(q0, q1):
-            o, i = T.OH[:, REP * q:REP * q + REP, 32 * j0:32 * j1], T.DR[:, :, 32 * j0:32 * j1]
+        for q in range(q0, q1, n):
+            o, i = T.OH[:, REP * q:REP * (q + n), 32 * j0:32 * j1], T.DR[:, 0:REP * n, 32 * j0:32 * j1]
             if e == "V":
                 fn = lambda: V.tensor_scalar(o, i, float(REP * q), None, A.is_equal)
             else:
                 fn = lambda: S.activation(o, i, AF.Sign, bias=con(q))
-            op(e, fn, r=["D0", "D1", "D2", "con0"] + ["D4_%d" % j for j in range(j0, j1)], w=["OH%d_%d" % (j, q) for j in range(j0, j1)])
+            op(e, fn, r=["D0", "D1", "D2", "D4", "D8"][:3 + n] + ["con0"], w=["OH%d_%d" % (j, k) for j in range(j0, j1) for k in range(q, q + n)])
+
+    def table_scalar(ch):
+        e, j0, j1, pb = ch
+        op("A", lambda: S.activation(T.dist[:, :], T.DR[:, 0:REP, 32 * j0:32 * j1], AF.Abs, bias=con(14)), r=["D0", "D1", "D2", "D4", "con14"], w=["dist"])
+        op("A", lambda: S.activation(T.OH[:, 64 - REP:64, 32 * j0:32 * j1], T.dist[:, :], AF.Relu, bias=con(13), scale=-1.0),
+           r=["dist", "con13"], w=["OH%d_7" % j0])
 
     def counts(ch):
         e, j0, j1, pb = ch
@@ -322,8 +319,8 @@ def rank_program(g, core, T, topo):
         def f():
             for G in range(2 * j0, 2 * j1):
                 ps, o = slice(64 * (G % 2), 64 * (G % 2) + 64), HC[pb] + 64 * (G // 2 - j0)
-                if e == "V":
-                    PE.matmul(T[pb][ps, o:o + 64], T.eye[:, ps], T.nb[:, 64 * (G // 2):64 * (G // 2) + 64], True, False)
+                if e == "V" and G % 2 == 0:
+                    PE.matmul(T[pb][:, o:o + 64], T.eye[:, :], T.nb[:, 32 * G:32 * G + 64], True, False)
                 for i in range(8):
                     k = 16 * G + 2 * i
                     if e == "V":
@@ -371,61 +368,59 @@ def rank_program(g, core, T, topo):
         else:
             op("A", lambda: S.activation(T.nb2[:, :], T.nb[:, :], AF.Identity, bias=con(8)), r=NB + ["con8"], w=["nb2"])
 
-    def uv_out(l, p, u):
-        o = (l * N + p) * 512 + 256 * u
-        return (T.UVl if p == rank else T.UVs)[:, o:o + 256]
+    def gather_uv(l, u, runs=((0, N),), q="A"):
+        for a, b in runs:
+            if a < b:
+                o = place(l, a, u).start
+                out, src = T.UVs[:, o:o + (b - a) * TK], (T.Uw, T.Vw)[u][:, :].indirect(T.woff[:, 16 * a:16 * b])
+                op(q, lambda: S.activation(out, src, AF.Copy) if q == "A" else V.tensor_copy(out, src),
+                   r=["Uw", "Vw", "woff"], w=["uv%d_%d_%d" % (l, u, p) for p in range(a, b)])
 
-    def gather_uv(l, p, u):
-        src = (T.Uw, T.Vw)[u][:, :].indirect(T.woff[:, 16 * p:16 * p + 16])
-        op("A", lambda: S.activation(uv_out(l, p, u), src, AF.Copy), r=["Uw", "Vw", "woff"], w=["uv%d_%d_%d" % (l, p, u)])
+    def two(p):
+        return ((p % N, p % N + 2),) if p % N < N - 1 else ((N - 1, N), (0, 1))
+
+    def cols(l, s, u):
+        return (T.UVs if s == rank else T.UVl)[:, place(l, s, u)]
 
     def have(l, s, u):
-        return ["uv%d_%d_%d" % (l, s, u)] if s == rank else ["far%d_%d_%d" % (l, s, u)]
+        return ["uv%d_%d_%d" % (l, u, s)] if s == rank else ["far%d_%d_%d" % (l, s, u)]
 
     Wof = lambda l, s: T.Wl[:, 256 * l + 64 * s:256 * l + 64 * s + 64]
 
     def winners_out(l):
-        op("V", lambda: V.tensor_scalar(Wof(l, rank), LP, 2048.0, None, A.subtract), r=["L"], w=["W%d_%d" % (l, rank)], b=["P0"])
+        op("V", lambda: V.tensor_scalar(Wof(l, rank), LP, 2048.0, None, A.subtract), r=["L"], w=["W%d_%d" % (l, rank)], b=["P2"])
         to_all(Wof(l, rank), "arrW%d_" % l + "%d", ["W%d_%d" % (l, rank)], "W%d_" % l + "%d")
 
     def winners_offsets():
-        op("V", lambda: V.tensor_copy(T.woff[:, :], LP), r=["L"], w=["woff"], b=["P0"])
+        op("V", lambda: V.tensor_copy(T.woff[:, :], LP), r=["L"], w=["woff"], b=["P2"])
 
     def shift_sums(l):
-        op("P", lambda: PE.matmul(yP, T.eyeH[:, :], T.nmH[:, :], True, False), r=["eyeH", "nmH"], w=["y"], b=["P2"])
-        for s in srcs:
-            def f():
-                for c in range(C):
-                    m = PE.matmul(T.P2[:, 128 + 64 * c:192 + 64 * c], T.eyeH[:, :], Wof(l, s), False, s == srcs[-1] and c == C - 1)
-                return m
-            op("P", f, r=["W%d_%d" % (l, s)], w=["y"], b=["P2"])
-
         def f():
             for n, s in enumerate(srcs):
                 m = PE.matmul(hP, T.eyeH[:, :], Wof(l, s), n == 0, n == N - 1)
             return m
-        op("P", f, r=["W%d_%d" % (l, s) for s in srcs], w=["h"], b=["P0"])
+        op("P", f, r=["W%d_%d" % (l, s) for s in srcs] + ["eyeH"], w=["h"], b=["P0"])
 
     def offsets(part):
         if part == 0:
-            op("V", lambda: V.tensor_scalar(T.tI[:, :], yP, 5 * 2048.0, None, A.add), r=["y"], w=["tI"], b=["P2"])
+            for c in range(C):
+                op("V", lambda: V.tensor_tensor(T.tI[:, 64 * c:64 * c + 64], T.nmH[:, 64 * c:64 * c + 64], hP, A.add), r=["h", "nmH"], w=["tI%d" % c], b=["P0"])
         elif part == 1:
-            op("V", lambda: V.tensor_scalar(T.tA[:, :], T.tI[:, :], E - 1, None, AND), r=["tI"], w=["tA"])
+            op("V", lambda: V.tensor_scalar(T.tA[:, :], T.tI[:, :], E - 1, None, AND), r=["tI%d" % c for c in range(C)], w=["tA"])
         else:
             op("V", lambda: V.tensor_copy(T.off[:, :], T.tA[:, :]), r=["tA"], w=["off"])
 
     def shift_tokens():
         for h in range(2):
             op("A", lambda: S.activation(T.Xh[:, h::2], hP, AF.Identity, scale=hmask[h]), r=["h"], w=["Xh%d" % h], b=["P0"])
-        op("P", lambda: PE.matmul(hT, T.Xh[:, :], T.rC[:, :], True, True), r=["Xh0", "Xh1", "rC"], w=["hT"], b=["P0"])
+        op("P", lambda: PE.matmul(hT, T.Xh[:, :], T.rC[:, :], True, True), r=["Xh0", "Xh1", "rC"], w=["hT"], b=["P2"])
 
     def f_prod(l, n):
         s = srcs[n]
-        o = (l * N + s) * 512
-        op("V", lambda: V.tensor_tensor(T.Pf[:, blk(s)], T.UVl[:, o:o + 256], xP, A.mult), r=have(l, s, 0) + ["xP"], w=["Pf%d" % s], b=["P1"])
+        op("V", lambda: V.tensor_tensor(T.Pf[:, blk(s)], cols(l, s, 0), xP, A.mult), r=have(l, s, 0) + ["xP"], w=["Pf%d" % s], b=["P1"])
 
-    def f_sum():
-        for n in FILL:
+    def f_sum(part):
+        for n in part:
             s = srcs[n]
 
             def f():
@@ -442,8 +437,10 @@ def rank_program(g, core, T, topo):
     def f_silu():
         op("V", lambda: V.tensor_tensor(T.sS[:, :], T.tt[:, :], dP, A.mult), r=["tt", "tt1", "d"], w=["sS"], b=["P5"])
 
-    def f_spread(n):
-        s, pb = srcs[n], "P%d" % (3 + n % 2)
+    MB, FB = ("P3", "P4", "P3", "P4"), ("P3", "P2", "P6", "P7")
+
+    def f_spread(n, banks=MB):
+        s, pb = srcs[n], banks[n]
 
         def f():
             for h in range(2):
@@ -453,27 +450,34 @@ def rank_program(g, core, T, topo):
         op("P", f, r=["sS", "bsel%d" % s, "bsel%d" % (4 + s)], w=["B%d" % s], b=[pb])
 
     def mix(l, n):
-        mm = T.mmF[:, 16:144] if l == RO - 1 else T.mmF[:, 0:128]
+        mm = T.mmF[:, 0:128]
         if n < 0:
             op("P", lambda: PE.matmul(uP, mm, T.xS[:, :], True, False), r=["mmF0", "mmF1", "xS"], w=["u"], b=["P5"])
         else:
             s = srcs[n]
             op("P", lambda: PE.matmul(uP, mm, T.Yf[:, blk(s)], False, n == N - 1), r=["Yf%d" % s], w=["u"], b=["P5"])
 
-    def f_y(l, n):
-        s, pb = srcs[n], "P%d" % (3 + n % 2)
-        o = (l * N + s) * 512 + 256
-        op("V", lambda: V.tensor_tensor(T.Yf[:, blk(s)], T.UVl[:, o:o + 256], T[pb][:, 256 * (n // 2):256 * (n // 2) + 256], A.mult),
-           r=have(l, s, 1) + ["B%d" % s], w=["Yf%d" % s], b=[pb])
+    def f_y(l, n, banks=MB, stay=False):
+        s, pb = srcs[n], banks[n]
+        B = T[pb][:, blk(n // 2)]
+        op("V", lambda: V.tensor_tensor(B if stay else T.Yf[:, blk(s)], cols(l, s, 1), B, A.mult),
+           r=have(l, s, 1) + ["B%d" % s], w=["B%d" % s if stay else "Yf%d" % s], b=[pb])
 
-    FB = ("P3", "P4", "P6", "P7")
+    def y_pair(n):
+        s, t, pb = srcs[n], srcs[n + 1], FB[n]
+        op("V", lambda: V.tensor_tensor(T.Yf[:, blk(t)], T.Yf[:, blk(t)], T[pb][:, blk(n // 2)], A.add), r=["B%d" % s, "Yf%d" % t], w=["Yf%d" % t], b=[pb])
 
-    def last_sum(n):
+    def add_x():
+        op("V", lambda: V.tensor_tensor(T.Yf[:, blk(rank)], T.Yf[:, blk(rank)], xP, A.add), r=["xP", "Yf%d" % rank], w=["Yf%d" % rank], b=["P1"])
+
+    def last_mix(n):
+        s = srcs[n]
+        op("P", lambda: PE.matmul(T.P4[:, 256:512], T.mmF[:, 16:144], T.Yf[:, blk(s)], n == 0, n == N - 1), r=["Yf%d" % s], w=["u"], b=["P4"])
+
+    def last_d(n):
         s, pb = srcs[n], FB[n]
+        f_prod(RO - 1, n)
         op("P", lambda: PE.matmul(T[pb][:, 0:256], T.quart[:, :], T.Pf[:, blk(s)], True, True), r=["Pf%d" % s, "quart"], w=["dl%d" % s], b=[pb])
-
-    def last_gate(n):
-        s, pb = srcs[n], FB[n]
         op("A", lambda: S.activation(T.t4[:, blk(s)], T[pb][:, 0:256], AF.Tanh, scale=2.0), r=["dl%d" % s], w=["t4%d" % s], b=[pb])
         op("A", lambda: S.activation(T.Pf[:, blk(s)], T.t4[:, blk(s)], AF.Identity, bias=con(13)), r=["t4%d" % s, "con13"], w=["Pf%d" % s])
 
@@ -483,22 +487,24 @@ def rank_program(g, core, T, topo):
 
     def last_y(n):
         s, pb, l = srcs[n], FB[n], RO - 1
-        o = (l * N + s) * 512 + 256
-        op("V", lambda: V.tensor_tensor(T.Yf[:, blk(s)], T.UVl[:, o:o + 256], T[pb][:, 256:512], A.mult), r=have(l, s, 1) + ["t5%d" % s], w=["Yf%d" % s], b=[pb])
+        op("V", lambda: V.tensor_tensor(T.Yf[:, blk(s)], cols(l, s, 1), T[pb][:, 256:512], A.mult), r=have(l, s, 1) + ["t5%d" % s], w=["Yf%d" % s], b=[pb])
 
     def f_tanh(l, parts=(0, 1)):
-        if l < RO - 1:
+        if l < 0:
+            if 0 in parts:
+                op("A", lambda: S.activation(xP, T.xB[:, :], AF.Copy), r=["xB"], w=["xP"], b=["P1"])
+            if 1 in parts:
+                op("A", lambda: S.activation(T.xS[:, :], T.xB[:, :], AF.Copy), r=["xB"], w=["xS"])
+        elif l < RO - 1:
             if 0 in parts:
                 op("A", lambda: S.activation(xP, uP, AF.Tanh, scale=0.5), r=["u"], w=["xP"], b=["P5", "P1"])
             if 1 in parts:
                 op("A", lambda: S.activation(T.xS[:, :], uP, AF.Tanh, scale=0.5), r=["u"], w=["xS"], b=["P5"])
         else:
-            op("A", lambda: S.activation(T.xo[:, :], uP, AF.Tanh, scale=0.5), r=["u"], w=["xo"], b=["P5"])
+            op("A", lambda: S.activation(T.xo[:, :], T.P4[:, 256:512], AF.Tanh, scale=0.5), r=["u"], w=["xo"], b=["P4"])
             dmas("A", "outx", [(T.yx[:, :], T.xo[:, :])], r=["xo"])
 
-    def x_start():
-        op("A", lambda: S.activation(xP, T.xB[:, :], AF.Copy), r=["xB"], w=["xP"], b=["P1"])
-        op("A", lambda: S.activation(T.xS[:, :], T.xB[:, :], AF.Copy), r=["xB"], w=["xS"])
+    def mixing_matrix():
         op("A", lambda: S.activation(T.mmF[:, 16:144], T.mmB[:, :], AF.Copy), r=["mmB"], w=["mmF0"])
         op("A", lambda: S.activation(T.mmF[:, 0:16], T.mmB[:, 112:128], AF.Copy), r=["mmB"], w=["mmF1"])
 
@@ -506,97 +512,89 @@ def rank_program(g, core, T, topo):
     for l in range(RO):
         last, x = l == RO - 1, l - 1
         if l == 0:
-            for s in srcs[1:]:
-                for c in (3, 2, 1):
-                    gather_raw(c, s * TK, s * TK + TK)
-            count_constants(0)
-            for c in range(C):
-                gather_mul(c, rank * TK, rank * TK + TK)
-            count_constants(1)
-            for s in srcs[1:]:
-                q_to_psum(s)
-                gather_mul(0, s * TK, s * TK + TK)
-                if s == srcs[-1]:
-                    scores(l, 0)
-                for c in (3, 2, 1):
-                    raw_mul(c, s * TK, s * TK + TK)
-                    if s == srcs[-1]:
-                        scores(l, c)
-            q_to_psum(rank)
+            for c in (3, 2, 1):
+                for a, b in ((0, rank * TK), (rank * TK + TK, 1024)):
+                    if a < b:
+                        gather_raw(c, a, b)
+            x_constants(0)
+            x_constants(1)
+            for n, c in FIRST:
+                s = srcs[n]
+                if c == 0:
+                    q_to_psum(s)
+                (gather_mul if c == 0 or n == 0 else raw_mul)(c, s * TK, s * TK + TK)
+                scores(l, c, s * TK, s * TK + TK)
             bias_cap(l)
         else:
             for part in RAW:
                 gather_raw(*part)
             gather_mul(0, 0, 1024)
             scores(l, 0)
-            gather_mul(1, 0, 256)
-            for k, part in enumerate(RAW):
-                raw_mul(*part)
-                if k % 2:
-                    scores(l, part[0])
-            if l > 1:
-                f_tanh(l - 2, (0,))
-            gather_uv(x, rank, 0)
-            if l > 1:
-                f_tanh(l - 2, (1,))
-            gather_uv(x, rank, 1)
+            gather_mul(1, 0, 512)
+            scores(l, 1, 0, 512)
+            for c in (3, 2):
+                raw_mul(c, 0, 512)
+                raw_mul(c, 512, 1024)
+                scores(l, c)
+            for a in (512, 768):
+                raw_mul(1, a, a + TK)
+                scores(l, 1, a, a + TK)
+            f_tanh(l - 2, (0,))
+            gather_uv(x, 1, two(rank - 1))
+            send_uv(x, SENDS[3:])
+            f_tanh(l - 2, (1,))
             bias_cap(l)
+            if l == 1:
+                mixing_matrix()
         select(l)
         if l > 0:
-            f_sum()
-        if last:
-            mix(x, -1)
+            f_sum(FILL[:3])
         to_list()
         shifted(1)
-        shifted(2)
         if l > 0:
-            f_gate()
+            f_prod(x, FILL[3])
+            f_sum(FILL[3:])
+        shifted(2)
+        shifted_far(4)
         if not last:
             c0, c1, c2, ca = MID
-            shifted_far(*ca[:3])
-            shifted_far("V", c0[1], c2[2])
-            tables(ca, 0, 8)
-            tables(c0, 0, 2)
+            tables(ca, 0, 1)
+            if l > 0:
+                f_gate()
+            tables(ca, 1, 2)
             winners_out(l)
+            tables(c0, 0, 1)
+            shifted_far(8)
+            tables(ca, 2, 8, 2)
+            table_scalar(c2)
+            tables(c0, 1, 3)
             if l > 0:
                 f_silu()
                 f_spread(0)
-            tables(c0, 2, 8)
+            tables(c0, 3, 8)
             counts(c0)
             if l > 0:
                 f_spread(1)
+            tables(c1, 0, 8)
             winners_offsets()
-            tables(c1, 0, 5)
-            new_bias(c0, 0)
-            tables(c1, 5, 8)
             counts(ca)
+            steps_out(ca)
             counts(c1)
-            if l == 0:
-                steps_out(ca)
-            for u in range(2):
-                gather_uv(l, peers[0], u)
-            if l > 0:
-                steps_out(ca)
-            to_home(l, [(0, 0, 2)])
-            tables(c2, 0, 5)
-            new_bias(c1, 1)
             differences(ca)
-            tables(c2, 5, 8)
+            tables(c2, 0, 7)
             counts(c2)
-            new_bias(ca, 2)
-            if l > 0:
-                f_y(x, 0)
-            new_bias(c2, 3)
+            for k, ch in enumerate((c0, c1, ca)):
+                new_bias(ch, k)
             if l > 0:
                 f_y(x, 1)
+            new_bias(c2, 3)
+            if l > 0:
+                f_y(x, 0)
             else:
-                x_constants(0)
-                x_constants(1)
-            for u in range(2):
-                gather_uv(l, peers[1], u)
+                x_constants(2)
+            gather_uv(l, 0)
+            gather_uv(l, 1, two(rank + 1))
             shift_sums(l)
-            for u in range(2):
-                gather_uv(l, peers[2], u)
             if l > 0:
                 f_spread(2)
                 f_spread(3)
@@ -610,55 +608,53 @@ def rank_program(g, core, T, topo):
                 f_y(x, 3)
                 for n in range(-1, N):
                     mix(x, n)
-            else:
-                x_constants(2)
-                x_start()
-            for k in range(1, N - 1):
-                to_home(l, [(k, 0, 2)], KB)
+            send_uv(l, SENDS[:3], KB)
         else:
             c0, c1 = END
-            shifted_far("V", 0, 4)
+            f_gate()
             winners_offsets()
-            for u in range(2):
-                for p in peers:
-                    gather_uv(l, p, u)
-            to_home(l, [(0, 0, 1), (1, 0, 1)])
-            to_home(l, [(2, 0, 1), (0, 1, 2)])
-            to_home(l, [(1, 1, 2), (2, 1, 2)])
+            gather_uv(l, 0, two(rank + 1))
+            gather_uv(l, 0, ((peers[2], peers[2] + 1),), "V")
             f_silu()
-            f_spread(0)
-            f_spread(1)
-            tables(c0, 0, 2)
+            gather_uv(l, 1, ((0, rank), (rank + 1, N)))
+            tables(c0, 0, 1)
+            send_uv(l, SENDS)
+            for u in range(2):
+                gather_uv(l, u, ((rank, rank + 1),))
             for n in range(N):
-                f_y(x, n)
-                if n < 2:
-                    f_spread(n + 2)
-                tables(c0, n + 2, n + 3)
-                mix(x, n)
-            gather_uv(l, rank, 0)
-            gather_uv(l, rank, 1)
-            f_tanh(x)
-            tables(c0, 6, 8)
+                f_spread(n, FB)
+            mix(x, -1)
+            tables(c0, 1, 2)
+            for n in (0, 2):
+                f_y(x, n, FB, True)
+                f_y(x, n + 1, FB)
+                tables(c0, n // 2 + 2, n // 2 + 3)
+                y_pair(n)
+                mix(x, n + 1)
+            f_tanh(x, (0,))
+            tables(c0, 4, 8)
+            last_d(0)
             counts(c0)
-            tables(c1, 0, 1)
-            for n in range(N):
-                f_prod(l, n)
-                last_sum(n)
-                last_gate(n)
-                tables(c1, 1 + 2 * n, min(3 + 2 * n, 8))
-                if n == 1:
-                    mix(l, -1)
-                if n > 0:
-                    last_silu(n - 1)
+            tables(c1, 0, 4)
+            last_d(1)
+            last_d(2)
+            last_silu(0)
+            tables(c1, 4, 5)
+            last_y(0)
+            last_d(3)
+            add_x()
+            last_mix(0)
+            tables(c1, 5, 8)
+            last_silu(1)
             counts(c1)
             last_bias(c0)
-            last_y(0)
-            last_silu(3)
-            for n in range(N):
-                if n > 0:
-                    last_y(n)
-                mix(l, n)
-            last_bias(c1)
+            for n in range(1, N):
+                last_y(n)
+                last_mix(n)
+                if n < N - 1:
+                    last_silu(n + 1)
+                if n == 2:
+                    last_bias(c1)
             f_tanh(l)
     for s in total:
         if max(seen[q].get(s, 0) for q in Q) < total[s]:

from concourse.bass import DstId, RemoteDMATransfer
from concourse.mybir import AluOpType, ActivationFunctionType

N, E, TK, C, RO = 4, 4096, 256, 4, 4
REP = 8
F32, BF, I32, U16, F16 = "float32", "bfloat16", "int32", "uint16", "float16"
MID = [("V", 0, 1, "P1"), ("V", 1, 2, "P2"), ("V", 2, 3, "P3"), ("A", 3, 4, "P4")]
END = [("V", 0, 2, "P0"), ("V", 2, 4, "P1")]
HC = {"P0": 384, "P1": 0, "P2": 0, "P3": 256, "P4": 256}
FILL = (0, 1, 2, 3)
RAW = [(3, 0, 1024), (2, 0, 1024), (1, 512, 1024)]
SENDS = ([(0, 0), (1, 0)], [(2, 0)], [(0, 1), (1, 1)], [(2, 1)])
FIRST = [(0, 0), (0, 1), (0, 2), (0, 3), (1, 0), (1, 3), (2, 0), (2, 3), (1, 2), (2, 2), (3, 0), (3, 3), (3, 2), (1, 1), (2, 1), (3, 1)]

SCRATCH = {
    "K": ("sbuf", [128, E], BF), "Uw": ("sbuf", [128, E], BF), "Vw": ("sbuf", [128, E], BF),
    "nmI": ("sbuf", [128, 256], I32), "nmC": ("sbuf", [128, 256], F32), "nmH": ("sbuf", [128, 256], F32), "qa": ("sbuf", [128, 1024], BF),
    "off": ("sbuf", [128, 256], U16), "woff": ("sbuf", [128, 64], U16), "tI": ("sbuf", [128, 256], I32), "tA": ("sbuf", [128, 256], I32),
    "prod": ("sbuf", [128, 4096], F16), "kraw": ("sbuf", [128, 4096], BF),
    "Xh": ("sbuf", [128, 128], F32), "X2": ("sbuf", [128, 512], F32),
    "run": ("sbuf", [128, 256], F32), "old": ("sbuf", [128, 256], F32), "win": ("sbuf", [128, 256], F32),
    "rst": ("sbuf", [128, 256], F32), "ci": ("sbuf", [128, 8, 8], I32), "DI": ("sbuf", [128, 64, 2], I32),
    "DR": ("sbuf", [128, 2 * REP, 128], BF), "X": ("sbuf", [128, 8, 32], BF), "OH": ("sbuf", [128, 65, 128], BF),
    "bias": ("sbuf", [128, 256], BF), "nb": ("sbuf", [128, 256], BF), "nb2": ("sbuf", [128, 256], BF),
    "nbF": ("sbuf", [128, 256], F32), "biasF": ("sbuf", [128, 256], F32), "Ss": ("sbuf", [128, 128], F32),
    "Wl": ("sbuf", [128, 3 * 256], F16), "UVs": ("sbuf", [128, RO * N * 512], BF), "UVl": ("sbuf", [128, RO * N * 512], BF),
    "xB": ("sbuf", [128, 256], BF), "xS": ("sbuf", [128, 256], F32), "xo": ("sbuf", [128, 256], F32),
    "mmB": ("sbuf", [128, 128], BF), "mmF": ("sbuf", [128, 144], F32),
    "Pf": ("sbuf", [128, 1024], F32), "Yf": ("sbuf", [128, 1024], F32), "tt": ("sbuf", [128, 128], F32), "sS": ("sbuf", [128, 128], F32),
    "pI": ("sbuf", [128, 2], I32), "cI": ("sbuf", [128, 12], I32), "cF": ("sbuf", [128, 12], F32), "cG": ("sbuf", [128, 12], F32),
    "Jn": ("sbuf", [128, 128], F32), "Jd": ("sbuf", [128, 192], F32), "Jb": ("sbuf", [128, 128], F32),
    "rS": ("sbuf", [128, 16], F16), "rC": ("sbuf", [128, 64], F32), "rL": ("sbuf", [128, 128], BF),
    "eye": ("sbuf", [128, 128], BF), "eyeH": ("sbuf", [128, 128], F16),
    "Dp": ("sbuf", [128, 128], F32), "Dn": ("sbuf", [128, 128], F32),
    "quart": ("sbuf", [128, 128], F32), "t4": ("sbuf", [128, 1024], F32),
    "dist": ("sbuf", [128, 256], BF), "con": ("sbuf", [128, 16], F32), "dsel": ("sbuf", [128, 192], F32), "bsel": ("sbuf", [128, 1024], F32),
}
for _b in range(8):
    SCRATCH["P%d" % _b] = ("psum", [128, 512], F32)
SEMAPHORES = (["cV", "cA", "cP", "cG", "ldq", "ldn", "ldk", "ldb", "ldx", "lduv", "bias0", "bias1", "bias2", "bias3", "outb", "outx", "sent", "sentq"]
              + ["arrq%d" % s for s in range(N)] + ["arrW%d_%d" % (l, s) for l in range(RO - 1) for s in range(N)]
              + ["arrU%d_%d_%d" % (l, s, u) for l in range(RO) for s in range(N) for u in range(2)])


def rank_program(g, core, T, topo):
    rank = T.rank_of(core)
    if rank is None:
        return
    A, AF = AluOpType, ActivationFunctionType
    Q = {"V": g.vector, "A": g.scalar, "P": g.tensor, "G": g, "S": g.sync}
    total, seen, lastw, readers, bank = {}, {k: {} for k in Q}, {}, {}, {}

    def need(q, ev):
        s, v = ev[0], ev[1]
        if seen[q].get(s, 0) < v:
            Q[q].wait_ge(T.sem[s], v)
            seen[q][s] = v

    def order(q, r, w, b, dma):
        evs = []
        for x in r:
            evs += [e for e in lastw.get(x, []) if dma or e[2] != q or q != "P"]
        for x in w:
            evs += [e for e in lastw.get(x, []) + readers.get(x, []) if dma or e[2] != q]
        for x in b:
            evs += [e for e in bank.get(x, {}).values() if e[2] != q]
        top = {}
        for e in evs:
            top[e[0]] = max(top.get(e[0], 0), e[1])
        for s in top:
            need(q, (s, top[s]))

    def note(ev, r, w, b):
        for x in r:
            readers.setdefault(x, []).append(ev)
        for x in w:
            lastw[x] = [ev]
            readers[x] = []
        for x in b:
            bank.setdefault(x, {})[ev[2]] = ev

    def op(q, fn, r=(), w=(), b=()):
        order(q, r, w, b, False)
        s = "c" + q
        total[s] = total.get(s, 0) + 1
        fn().then_inc(T.sem[s], 1)
        note((s, total[s], q), r, w, b)

    def dmas(q, sem, pairs, r=(), w=()):
        order(q, r, w, (), True)
        for o, i in pairs:
            Q[q].dma_start(o, i).then_inc(T.sem[sem], 16)
        total[sem] = total.get(sem, 0) + 16 * len(pairs)
        note((sem, total[sem], "dma"), r, w, ())

    def arrives(sem, n, w):
        total[sem] = total.get(sem, 0) + n
        lastw[w] = [(sem, total[sem], "far")]

    peers = [(rank + k) % N for k in range(1, N)]
    srcs = [rank] + peers[::-1]
    eng = [e for e in topo.engines(core, T.cores[peers[0]]) if all(e in topo.engines(core, T.cores[p]) for p in peers)]
    assert all(topo.may_write(core, T.cores[p]) for p in peers) and len(eng) >= 8
    eng = eng[:8]

    def bits(es):
        return sum(1 << e for e in es)

    def dst(p):
        a = topo.addr(T.cores[p])
        return DstId(rid=a[0], pnc=a[1])

    def to_all(ap, sem, r, name, left="sent"):
        order("G", r, (), (), True)
        g.remote_dma_fused([RemoteDMATransfer(dst_ids=[dst(p) for p in peers], dma_engine_mask=bits(eng), remote_sem=T.sem[sem % rank],
                                              srcs=[ap], dsts=[ap] * len(peers))], local_sem=T.sem[left])
        total[left] = total.get(left, 0) + len(eng)
        for p in peers:
            arrives(sem % p, len(eng), name % p)

    def place(l, s, u):
        o = ((2 * l + u) * N + s) * TK
        return slice(o, o + TK)

    def send_uv(l, calls, more=()):
        for parts in calls:
            trs = []
            for j, (k, u) in enumerate(parts):
                p, s, e = peers[k], (rank - k - 1) % N, eng[j::len(parts)]
                order("G", ["uv%d_%d_%d" % (l, u, p)] + list(more), (), (), True)
                trs.append(RemoteDMATransfer(dst_ids=[dst(p)], dma_engine_mask=bits(e), remote_sem=T.sem["arrU%d_%d_%d" % (l, rank, u)],
                                             src=T.UVs[:, place(l, p, u)], dst=T.UVl[:, place(l, rank, u)]))
                total["sent"] = total.get("sent", 0) + len(e)
                arrives("arrU%d_%d_%d" % (l, s, u), len(e), "far%d_%d_%d" % (l, s, u))
            g.remote_dma_fused(trs, local_sem=T.sem.sent)

    V, S, PE = g.vector, g.scalar, g.tensor
    SC, NM, hT, LP, hP = T.P0[:, 0:256], T.P0[:, 256:512], T.P2[:, 384:448], T.P2[:, 448:512], T.P0[:, 0:64]
    xP = T.P1[:, 256:512]
    dP, uP = T.P5[:, 0:128], T.P5[:, 256:512]
    KB, NB, QS = ["Kb%d" % j for j in range(4)], ["nb%d" % j for j in range(4)], ["q%d" % s for s in range(N)]

    def turned(d, s):
        return [(d[16:128, :], s[0:112, :]), (d[0:16, :], s[112:128, :])]

    def bias_rows(t, rows, j0, j1):
        out = []
        for j in range(j0, j1):
            if j == 0:
                out += [(t[0:64, 0:64], rows(7, 7)), (t[64:128, 0:64], rows(0, 0))]
            else:
                out.append((t[:, 64 * j:64 * j + 64], rows(2 * j - 1, 2 * j)))
        return out

    blk = lambda s: slice(s * TK, (s + 1) * TK)
    dmas("S", "ldq", [(T.qa[:, blk(rank)], T.rq[:, :])], w=["q%d" % rank])
    dmas("S", "ldk", [(T.K[:, :], T.ke[:, :])], w=["K"])
    dmas("A", "ldn", [(T.nmI[:, :], T.nm[:, :])], w=["nmI"])
    kerows = lambda a, b: T.ke[16 * a + 15:16 * b + 16:16, :]
    flt = dict(allow_small_or_imprecise_dtypes=True)
    op("G", lambda: g.iota(T.pI[:, :], [[16, 2]], 0, 1), w=["pI"])
    op("G", lambda: g.iota(T.Jn[:, :], [[1, 128]], 0, 0, **flt), w=["Jn"])
    op("G", lambda: g.iota(T.Jb[:, :], [[1, 8], [0, 16]], 0, 0, **flt), w=["Jb"])
    op("G", lambda: g.iota(T.Jd[:, :], [[0, 3], [1, 64]], 0, 0, **flt), w=["Jd"])
    to_all(T.qa[:, blk(rank)], "arrq%d", ["q%d" % rank], "q%d", "sentq")
    lastw["qleft"] = [("sentq", total["sentq"], "far")]
    SR, AND = A.arith_shift_right, A.bitwise_and
    p0, p16 = T.pI[:, 0:1], T.pI[:, 1:2]
    cf = lambda j: T.cF[:, j:j + 1]
    cg = lambda j: T.cG[:, j:j + 1]
    con = lambda j: T.con[:, j:j + 1]
    for j, v in ((10, 20.0), (8, 2.0), (9, 4.0), (13, 1.0), (14, -56.0)):
        op("V", lambda: V.memset(con(j), v), w=["con%d" % j])
    op("A", lambda: S.activation(T.tt[64:128, :], T.Jn[64:128, :], AF.Tanh, bias=T.con[64:128, 10:11]), r=["Jn", "con10"], w=["tt1"])
    cuts = [(p0, 4, 7), (p0, 0, 63), (p0, 0, 7), (p16, 4, 7), (p0, 3, 1), (p0, 0, 1), (p0, 1, 63), (p0, 0, 127), (p0, 0, 15)]
    for j, (src, sh, m) in enumerate(cuts):
        op("V", lambda: V.tensor_scalar(T.cI[:, j:j + 1], src, sh, m, SR, AND), r=["pI"], w=["cI%d" % j])
    op("V", lambda: V.tensor_copy(T.cF[:, 0:9], T.cI[:, 0:9]), r=["cI%d" % j for j in range(9)], w=["cF"])
    op("V", lambda: V.memset(T.old[:, 0:1], 0.0), w=["old0"])
    op("V", lambda: V.tensor_scalar(cg(0), cf(3), 8.0, cf(2), A.mult, A.add), r=["cF"], w=["cG0"])
    op("V", lambda: V.tensor_scalar(T.cG[:, 2:4], T.cF[:, 4:6], 0.0, None, A.is_equal), r=["cF"], w=["cG2"])
    op("V", lambda: V.tensor_scalar(cg(1), cg(0), 131072.0, None, A.mult), r=["cG0"], w=["cG1"])
    op("V", lambda: V.tensor_scalar(T.rC[:, :], T.Jn[:, 0:64], cg(0), None, A.is_equal), r=["cG0", "Jn"], w=["rC"])
    op("V", lambda: V.tensor_copy(T.off[:, :], T.nmI[:, :]), r=["nmI"], w=["off"])
    for c in range(C):
        op("V", lambda: V.tensor_scalar(T.nmC[:, 64 * c:64 * c + 64], T.nmI[:, 64 * c:64 * c + 64], cg(1), float((3 - c) * 32768 + 8192), A.add, A.add),
           r=["nmI", "cG1"], w=["nmC%d" % c])
    op("V", lambda: V.tensor_scalar(T.eye[:, :], T.Jn[:, :], cf(7), None, A.is_equal), r=["cF", "Jn"], w=["eye"])
    op("V", lambda: V.memset(T.rst[:, :], 0.0), w=["rst0"])
    op("V", lambda: V.tensor_scalar(T.rS[:, 0:8], T.Jn[:, 0:8], cf(3), None, A.is_equal), r=["cF", "Jn"], w=["rS0"])
    op("V", lambda: V.memset(T.rst[:, 0::4], -100000.0), r=["rst0"], w=["rst"])
    op("V", lambda: V.tensor_scalar(T.rL[:, 0:64], T.Jn[:, 0:64], cf(6), 64.0, A.is_equal, A.mult), r=["cF", "Jn"], w=["rL0"])
    op("V", lambda: V.tensor_scalar(T.rL[:, 64:128], T.Jn[:, 0:64], cf(6), None, A.is_equal), r=["cF", "Jn"], w=["rL1"])
    op("V", lambda: V.tensor_scalar(T.con[:, 0:8], T.Jn[:, 0:8], -float(REP), 0.5, A.mult, A.add), r=["Jn"], w=["con0"])

    op("V", lambda: V.tensor_scalar(cg(6), cf(8), 15.0, -2.0, A.is_equal, A.mult), r=["cF"], w=["cG6"])
    op("V", lambda: V.tensor_scalar(T.nmH[:, :], T.nmI[:, :], 4 * 2048.0, None, A.add), r=["nmI"], w=["nmH"])
    op("V", lambda: V.tensor_scalar(cg(7), cg(6), 1.0, None, A.add), r=["cG6"], w=["cG7"])
    op("V", lambda: V.tensor_scalar(T.eyeH[:, :], T.eye[:, :], 1.0, None, A.mult), r=["eye"], w=["eyeH"])
    op("V", lambda: V.memset(T.OH[:, 64], -1.0), w=["OHend"])
    op("V", lambda: V.tensor_scalar(T.rS[:, 8:16], T.Jn[:, 0:8], cf(3), cg(7), A.is_equal, A.mult), r=["cF", "Jn", "cG7"], w=["rS1"])
    for D, name, v in ((T.Dp, "Dp", 0.25), (T.Dn, "Dn", -0.25)):
        op("G", lambda: g.iota(D[:, :], [[0, 128]], 0, 0, **flt), w=[name])
        for fill, step, base, cm in ((v, -1, 0, 1), (-v, -1, -1, 1), (0.0, 1, -64 * 128 - 63, 128), (v, 1, -63, 128), (v, 1, -64 * 128 - 127, 128)):
            op("G", lambda: g.affine_select(D[:, :], D[:, :], [[step, 128]], A.not_equal, fill, base, cm), r=[name], w=[name])

    def x_constants(part):
        if part == 0:
            op("V", lambda: V.tensor_scalar(cg(10), cf(0), 56.0, None, A.add), r=["cF"], w=["cG10"])
            op("V", lambda: V.tensor_scalar(T.quart[:, :], T.Jb[:, :], cf(0), 0.25, A.is_equal, A.mult), r=["Jb", "cF"], w=["quart"])
            op("V", lambda: V.tensor_scalar(T.dsel[:, :], T.Jd[:, :], cg(10), 0.25, A.is_equal, A.mult), r=["Jd", "cG10"], w=["dsel"])
            return
        for k in range(4 * part - 4, 4 * part):
            op("V", lambda: V.tensor_scalar(T.bsel[:, 128 * k:128 * k + 128], T.Jb[:, :], float(8 * k), cf(1), A.add, A.is_equal), r=["Jb", "cF"], w=["bsel%d" % k])

    dmas("S", "ldb", bias_rows(T.bias, kerows, 0, 4), r=["K"], w=["bias"])
    dmas("S", "lduv", turned(T.Uw, T.ue) + turned(T.Vw, T.ve), r=["qleft"], w=["Uw", "Vw"])
    dmas("S", "ldx", turned(T.xB, T.x0) + turned(T.mmB, T.mm), w=["xB", "mmB"])

    hmask = (cg(2), cf(4))
    pmask = (cg(3), cf(5))

    def names():
        for h in range(2):
            op("A", lambda: S.activation(T.X2[:, h::2], T.nmC[:, :], AF.Identity, scale=hmask[h]),
               r=["nmC%d" % c for c in range(C)] + ["cG2", "cF"], w=["X2%d" % h])

        def f():
            for c in range(C):
                m = PE.matmul(T.P0[:, 256 + c:512:4], T.X2[:, 128 * c:128 * c + 128], T.rC[:, :], True, True)
            return m
        op("P", f, r=["X20", "X21", "rC"], w=["names"], b=["P0"])

    def q_to_psum(s):
        pb = "P%d" % (6 + s // 2)
        op("P", lambda: PE.matmul(T[pb][:, 256 * (s % 2):256 * (s % 2) + 256], T.eye[:, :], T.qa[:, blk(s)], True, True), r=["eye", "q%d" % s], w=["qP%d" % s], b=[pb])

    def pieces(c, a, b):
        return ["pr%d_%d" % (c, s) for s in range(a // TK, b // TK)]

    def scores(l, c, a=0, b=1024):
        rs = T.rS[:, 0:8] if l == 0 else T.rS[:, 8:16]

        def f():
            for i in range(8):
                m = PE.matmul(T.P0[a // 8:b // 8, 4 * i + c:256:32], T.prod[:, 1024 * c + a + i:1024 * c + b:8], rs, True, True)
            return m
        op("P", f, r=pieces(c, a, b) + ["rS%d" % min(l, 1)], w=["S" + x for x in pieces(c, a, b)], b=["P0"])

    def keys(c, a, b):
        return T.K[:, :].indirect(T.off[:, 64 * c + a // 16:64 * c + b // 16])

    def gather_mul(c, a, b):
        op("V", lambda: V.tensor_tensor(T.prod[:, 1024 * c + a:1024 * c + b], keys(c, a, b), T.qa[:, a:b], A.mult),
           r=["K", "off"] + KB + QS[a // TK:b // TK], w=pieces(c, a, b))

    def gather_raw(c, a, b):
        op("A", lambda: S.activation(T.kraw[:, 1024 * c + a:1024 * c + b], keys(c, a, b), AF.Copy),
           r=["K", "off"] + KB, w=["raw" + x for x in pieces(c, a, b)])

    def raw_mul(c, a, b):
        pb, o = "P%d" % (6 + a // 512), a % 512
        op("V", lambda: V.tensor_tensor(T.prod[:, 1024 * c + a:1024 * c + b], T.kraw[:, 1024 * c + a:1024 * c + b], T[pb][:, o:o + b - a], A.mult),
           r=["raw" + x for x in pieces(c, a, b)] + ["qP%d" % s for s in range(a // TK, b // TK)], w=pieces(c, a, b), b=[pb])

    def select(l):
        ss = ["S" + x for c in range(C) for x in pieces(c, 0, 1024)]
        fill = (lambda n: f_prod(l - 1, FILL[n])) if l > 0 else (lambda n: None)
        fill(0)
        op("V", lambda: V.tensor_tensor_scan(T.run[:, :], T.rst[:, :], SC, 0.0, A.add, A.max), r=ss + ["rst"], w=["run"], b=["P0"])
        fill(1)
        op("V", lambda: V.tensor_tensor(T.old[:, 1:256], T.P0[:, 1:256], T.run[:, 0:255], A.is_le), r=ss + ["run"], w=["old"], b=["P0"])
        fill(2)
        op("V", lambda: V.tensor_tensor_scan(T.win[:, :], T.old[:, :], NM, 0.0, A.mult, A.max), r=["old", "old0", "names"], w=["win"], b=["P0"])
        if l == 0:
            op("V", lambda: V.tensor_copy(T.ci[:, :, :], T.win[:, 3::4]), r=["win"], w=["ci"])
        else:
            op("V", lambda: V.tensor_tensor(T.ci[:, :, :], T.win[:, 3::4], hT, A.add), r=["win", "hT"], w=["ci"], b=["P2"])
        op("V", lambda: V.tensor_scalar(T.DI[:, :, 0], T.ci[:, :, :], 6, 63, SR, AND), r=["ci"], w=["DI0"])
        op("V", lambda: V.tensor_scalar(T.DI[:, :, 1], T.ci[:, :, :], 63, None, AND), r=["ci"], w=["DI1"])
        op("V", lambda: V.tensor_copy(T.DR[:, 0], T.DI[:, :, :]), r=["DI0", "DI1"], w=["D0"])

    def to_list():
        for h in range(2):
            op("A", lambda: S.activation(T.X[:, :, 16 * h:16 * h + 16], T.DR[:, 0], AF.Identity, scale=pmask[h]), r=["D0", "cG2", "cF"], w=["X%d" % h])

        def f():
            for d in range(2):
                m = PE.matmul(LP, T.X[:, :, d::2], T.rL[:, 64 * d:64 * d + 64], d == 0, d == 1)
            return m
        op("P", f, r=["X0", "X1", "rL0", "rL1"], w=["L"], b=["P2"])

    def shifted(n):
        op("V", lambda: V.tensor_scalar(T.DR[:, n:2 * n], T.DR[:, 0:n], float(n), None, A.subtract), r=["D0", "D1"][:n], w=["D%d" % n])

    def shifted_far(n):
        cs = slice(0, 128) if n == 4 else slice(96, 128)
        op("V", lambda: V.tensor_scalar(T.DR[:, n:2 * n, cs], T.DR[:, 0:n, cs], float(n), None, A.subtract), r=["D0", "D1", "D2", "D4"][:2 + n // 4], w=["D%d" % n])

    def tables(ch, q0, q1, n=1):
        e, j0, j1, pb = ch
        for q in range(q0, q1, n):
            o, i = T.OH[:, REP * q:REP * (q + n), 32 * j0:32 * j1], T.DR[:, 0:REP * n, 32 * j0:32 * j1]
            if e == "V":
                fn = lambda: V.tensor_scalar(o, i, float(REP * q), None, A.is_equal)
            else:
                fn = lambda: S.activation(o, i, AF.Sign, bias=con(q))
            op(e, fn, r=["D0", "D1", "D2", "D4", "D8"][:3 + n] + ["con0"], w=["OH%d_%d" % (j, k) for j in range(j0, j1) for k in range(q, q + n)])

    def table_scalar(ch):
        e, j0, j1, pb = ch
        op("A", lambda: S.activation(T.dist[:, :], T.DR[:, 0:REP, 32 * j0:32 * j1], AF.Abs, bias=con(14)), r=["D0", "D1", "D2", "D4", "con14"], w=["dist"])
        op("A", lambda: S.activation(T.OH[:, 64 - REP:64, 32 * j0:32 * j1], T.dist[:, :], AF.Relu, bias=con(13), scale=-1.0),
           r=["dist", "con13"], w=["OH%d_7" % j0])

    def counts(ch):
        e, j0, j1, pb = ch

        def f():
            for G in range(2 * j0, 2 * j1):
                ps, o = slice(64 * (G % 2), 64 * (G % 2) + 64), HC[pb] + 64 * (G // 2 - j0)
                if e == "V" and G % 2 == 0:
                    PE.matmul(T[pb][:, o:o + 64], T.eye[:, :], T.nb[:, 32 * G:32 * G + 64], True, False)
                for i in range(8):
                    k = 16 * G + 2 * i
                    if e == "V":
                        m = PE.matmul(T[pb][ps, o:o + 64], T.OH[:, 0:64, k], T.OH[:, 0:64, k + 1], False, i == 7)
                    else:
                        m = PE.matmul(T.P5[ps, 128:193], T.OH[:, 0:64, k], T.OH[:, :, k + 1], i == 0, i == 7)
            return m
        op("P", f, r=["OH%d_%d" % (j, q) for j in range(j0, j1) for q in range(64 // REP)] + NB[j0:j1] + ["eye", "OHend"],
           w=["H%d" % j for j in range(j0, j1)], b=[pb if e == "V" else "P5"])

    def steps_out(ch):
        op("A", lambda: S.activation(T.Ss[:, 0:65], T.P5[:, 128:193], AF.Copy), r=["H%d" % ch[1]], w=["Ss"], b=["P5"])

    def differences(ch):
        e, j0, j1, pb = ch
        H = T[pb][:, HC[pb]:HC[pb] + 64]

        def f():
            PE.matmul(H, T.eye[:, :], T.nb[:, 64 * j0:64 * j1], True, False)
            PE.matmul(H, T.Dp[:, :], T.Ss[:, 0:64], False, False)
            return PE.matmul(H, T.Dn[:, :], T.Ss[:, 1:65], False, True)
        op("P", f, r=["Ss", "Dp", "Dn", "eye", "nb%d" % j0], w=["H%d" % j0], b=[pb])

    def new_bias(ch, k):
        e, j0, j1, pb = ch
        cs, js = slice(64 * j0, 64 * j1), range(j0, j1)
        op("V", lambda: V.tensor_tensor(T.nb[:, cs], T[pb][:, HC[pb]:HC[pb] + 64 * (j1 - j0)], T.nb2[:, cs], A.min),
           r=["H%d" % j for j in js] + ["nb2"], w=NB[j0:j1], b=[pb])
        rows = lambda a, b: T.K[16 * a + 15:16 * b + 16:16, :]
        dmas("S", "bias%d" % k, [(o, i) for i, o in bias_rows(T.nb, rows, j0, j1)], r=NB[j0:j1], w=KB[j0:j1])

    def last_bias(ch):
        e, j0, j1, pb = ch
        cs, js = slice(64 * j0, 64 * j1), range(j0, j1)
        op("V", lambda: V.tensor_tensor(T.nbF[:, cs], T[pb][:, HC[pb]:HC[pb] + 64 * (j1 - j0)], T.nb2[:, cs], A.min),
           r=["H%d" % j for j in js] + ["nb2"], w=["nbF%d" % j0], b=[pb])
        op("A", lambda: S.activation(T.biasF[:, cs], T.nbF[:, cs], AF.Identity, bias=con(9), scale=-1.0), r=["nbF%d" % j0, "con9"], w=["bF%d" % j0])
        rows = lambda a, b: T.yb[a:b + 1, :]
        dmas("S", "outb", [(o, i) for i, o in bias_rows(T.biasF, rows, j0, j1)], r=["bF%d" % j0])

    def bias_cap(l):
        if l == 0:
            op("A", lambda: S.activation(T.nb[:, :], T.bias[:, :], AF.Identity, scale=-1.0), r=["bias"], w=NB)
            op("A", lambda: S.activation(T.nb2[:, :], T.bias[:, :], AF.Identity, bias=con(8), scale=-1.0), r=["bias", "con8"], w=["nb2"])
        else:
            op("A", lambda: S.activation(T.nb2[:, :], T.nb[:, :], AF.Identity, bias=con(8)), r=NB + ["con8"], w=["nb2"])

    def gather_uv(l, u, runs=((0, N),), q="A"):
        for a, b in runs:
            if a < b:
                o = place(l, a, u).start
                out, src = T.UVs[:, o:o + (b - a) * TK], (T.Uw, T.Vw)[u][:, :].indirect(T.woff[:, 16 * a:16 * b])
                op(q, lambda: S.activation(out, src, AF.Copy) if q == "A" else V.tensor_copy(out, src),
                   r=["Uw", "Vw", "woff"], w=["uv%d_%d_%d" % (l, u, p) for p in range(a, b)])

    def two(p):
        return ((p % N, p % N + 2),) if p % N < N - 1 else ((N - 1, N), (0, 1))

    def cols(l, s, u):
        return (T.UVs if s == rank else T.UVl)[:, place(l, s, u)]

    def have(l, s, u):
        return ["uv%d_%d_%d" % (l, u, s)] if s == rank else ["far%d_%d_%d" % (l, s, u)]

    Wof = lambda l, s: T.Wl[:, 256 * l + 64 * s:256 * l + 64 * s + 64]

    def winners_out(l):
        op("V", lambda: V.tensor_scalar(Wof(l, rank), LP, 2048.0, None, A.subtract), r=["L"], w=["W%d_%d" % (l, rank)], b=["P2"])
        to_all(Wof(l, rank), "arrW%d_" % l + "%d", ["W%d_%d" % (l, rank)], "W%d_" % l + "%d")

    def winners_offsets():
        op("V", lambda: V.tensor_copy(T.woff[:, :], LP), r=["L"], w=["woff"], b=["P2"])

    def shift_sums(l):
        def f():
            for n, s in enumerate(srcs):
                m = PE.matmul(hP, T.eyeH[:, :], Wof(l, s), n == 0, n == N - 1)
            return m
        op("P", f, r=["W%d_%d" % (l, s) for s in srcs] + ["eyeH"], w=["h"], b=["P0"])

    def offsets(part):
        if part == 0:
            for c in range(C):
                op("V", lambda: V.tensor_tensor(T.tI[:, 64 * c:64 * c + 64], T.nmH[:, 64 * c:64 * c + 64], hP, A.add), r=["h", "nmH"], w=["tI%d" % c], b=["P0"])
        elif part == 1:
            op("V", lambda: V.tensor_scalar(T.tA[:, :], T.tI[:, :], E - 1, None, AND), r=["tI%d" % c for c in range(C)], w=["tA"])
        else:
            op("V", lambda: V.tensor_copy(T.off[:, :], T.tA[:, :]), r=["tA"], w=["off"])

    def shift_tokens():
        for h in range(2):
            op("A", lambda: S.activation(T.Xh[:, h::2], hP, AF.Identity, scale=hmask[h]), r=["h"], w=["Xh%d" % h], b=["P0"])
        op("P", lambda: PE.matmul(hT, T.Xh[:, :], T.rC[:, :], True, True), r=["Xh0", "Xh1", "rC"], w=["hT"], b=["P2"])

    def f_prod(l, n):
        s = srcs[n]
        op("V", lambda: V.tensor_tensor(T.Pf[:, blk(s)], cols(l, s, 0), xP, A.mult), r=have(l, s, 0) + ["xP"], w=["Pf%d" % s], b=["P1"])

    def f_sum(part):
        for n in part:
            s = srcs[n]

            def f():
                for h in range(2):
                    k = 4 * h + s
                    m = PE.matmul(dP, T.dsel[:, 56 - 8 * k:184 - 8 * k], T.Pf[:, 256 * s + 128 * h:256 * s + 128 * h + 128],
                                  n == FILL[0] and h == 0, n == FILL[-1] and h == 1)
                return m
            op("P", f, r=["Pf%d" % s, "dsel"], w=["d"], b=["P5"])

    def f_gate():
        op("A", lambda: S.activation(T.tt[0:64, :], T.P5[0:64, 0:128], AF.Tanh, scale=2.0), r=["d"], w=["tt"], b=["P5"])

    def f_silu():
        op("V", lambda: V.tensor_tensor(T.sS[:, :], T.tt[:, :], dP, A.mult), r=["tt", "tt1", "d"], w=["sS"], b=["P5"])

    MB, FB = ("P3", "P4", "P3", "P4"), ("P3", "P2", "P6", "P7")

    def f_spread(n, banks=MB):
        s, pb = srcs[n], banks[n]

        def f():
            for h in range(2):
                k, o = 4 * h + s, 256 * (n // 2) + 128 * h
                m = PE.matmul(T[pb][:, o:o + 128], T.bsel[:, 128 * k:128 * k + 128], T.sS[:, :], True, True)
            return m
        op("P", f, r=["sS", "bsel%d" % s, "bsel%d" % (4 + s)], w=["B%d" % s], b=[pb])

    def mix(l, n):
        mm = T.mmF[:, 0:128]
        if n < 0:
            op("P", lambda: PE.matmul(uP, mm, T.xS[:, :], True, False), r=["mmF0", "mmF1", "xS"], w=["u"], b=["P5"])
        else:
            s = srcs[n]
            op("P", lambda: PE.matmul(uP, mm, T.Yf[:, blk(s)], False, n == N - 1), r=["Yf%d" % s], w=["u"], b=["P5"])

    def f_y(l, n, banks=MB, stay=False):
        s, pb = srcs[n], banks[n]
        B = T[pb][:, blk(n // 2)]
        op("V", lambda: V.tensor_tensor(B if stay else T.Yf[:, blk(s)], cols(l, s, 1), B, A.mult),
           r=have(l, s, 1) + ["B%d" % s], w=["B%d" % s if stay else "Yf%d" % s], b=[pb])

    def y_pair(n):
        s, t, pb = srcs[n], srcs[n + 1], FB[n]
        op("V", lambda: V.tensor_tensor(T.Yf[:, blk(t)], T.Yf[:, blk(t)], T[pb][:, blk(n // 2)], A.add), r=["B%d" % s, "Yf%d" % t], w=["Yf%d" % t], b=[pb])

    def add_x():
        op("V", lambda: V.tensor_tensor(T.Yf[:, blk(rank)], T.Yf[:, blk(rank)], xP, A.add), r=["xP", "Yf%d" % rank], w=["Yf%d" % rank], b=["P1"])

    def last_mix(n):
        s = srcs[n]
        op("P", lambda: PE.matmul(T.P4[:, 256:512], T.mmF[:, 16:144], T.Yf[:, blk(s)], n == 0, n == N - 1), r=["Yf%d" % s], w=["u"], b=["P4"])

    def last_d(n):
        s, pb = srcs[n], FB[n]
        f_prod(RO - 1, n)
        op("P", lambda: PE.matmul(T[pb][:, 0:256], T.quart[:, :], T.Pf[:, blk(s)], True, True), r=["Pf%d" % s, "quart"], w=["dl%d" % s], b=[pb])
        op("A", lambda: S.activation(T.t4[:, blk(s)], T[pb][:, 0:256], AF.Tanh, scale=2.0), r=["dl%d" % s], w=["t4%d" % s], b=[pb])
        op("A", lambda: S.activation(T.Pf[:, blk(s)], T.t4[:, blk(s)], AF.Identity, bias=con(13)), r=["t4%d" % s, "con13"], w=["Pf%d" % s])

    def last_silu(n):
        s, pb = srcs[n], FB[n]
        op("V", lambda: V.tensor_tensor(T[pb][:, 256:512], T.Pf[:, blk(s)], T[pb][:, 0:256], A.mult), r=["Pf%d" % s, "dl%d" % s], w=["t5%d" % s], b=[pb])

    def last_y(n):
        s, pb, l = srcs[n], FB[n], RO - 1
        op("V", lambda: V.tensor_tensor(T.Yf[:, blk(s)], cols(l, s, 1), T[pb][:, 256:512], A.mult), r=have(l, s, 1) + ["t5%d" % s], w=["Yf%d" % s], b=[pb])

    def f_tanh(l, parts=(0, 1)):
        if l < 0:
            if 0 in parts:
                op("A", lambda: S.activation(xP, T.xB[:, :], AF.Copy), r=["xB"], w=["xP"], b=["P1"])
            if 1 in parts:
                op("A", lambda: S.activation(T.xS[:, :], T.xB[:, :], AF.Copy), r=["xB"], w=["xS"])
        elif l < RO - 1:
            if 0 in parts:
                op("A", lambda: S.activation(xP, uP, AF.Tanh, scale=0.5), r=["u"], w=["xP"], b=["P5", "P1"])
            if 1 in parts:
                op("A", lambda: S.activation(T.xS[:, :], uP, AF.Tanh, scale=0.5), r=["u"], w=["xS"], b=["P5"])
        else:
            op("A", lambda: S.activation(T.xo[:, :], T.P4[:, 256:512], AF.Tanh, scale=0.5), r=["u"], w=["xo"], b=["P4"])
            dmas("A", "outx", [(T.yx[:, :], T.xo[:, :])], r=["xo"])

    def mixing_matrix():
        op("A", lambda: S.activation(T.mmF[:, 16:144], T.mmB[:, :], AF.Copy), r=["mmB"], w=["mmF0"])
        op("A", lambda: S.activation(T.mmF[:, 0:16], T.mmB[:, 112:128], AF.Copy), r=["mmB"], w=["mmF1"])

    names()
    for l in range(RO):
        last, x = l == RO - 1, l - 1
        if l == 0:
            for c in (3, 2, 1):
                for a, b in ((0, rank * TK), (rank * TK + TK, 1024)):
                    if a < b:
                        gather_raw(c, a, b)
            x_constants(0)
            x_constants(1)
            for n, c in FIRST:
                s = srcs[n]
                if c == 0:
                    q_to_psum(s)
                (gather_mul if c == 0 or n == 0 else raw_mul)(c, s * TK, s * TK + TK)
                scores(l, c, s * TK, s * TK + TK)
            bias_cap(l)
        else:
            for part in RAW:
                gather_raw(*part)
            gather_mul(0, 0, 1024)
            scores(l, 0)
            gather_mul(1, 0, 512)
            scores(l, 1, 0, 512)
            for c in (3, 2):
                raw_mul(c, 0, 512)
                raw_mul(c, 512, 1024)
                scores(l, c)
            for a in (512, 768):
                raw_mul(1, a, a + TK)
                scores(l, 1, a, a + TK)
            f_tanh(l - 2, (0,))
            gather_uv(x, 1, two(rank - 1))
            send_uv(x, SENDS[3:])
            f_tanh(l - 2, (1,))
            bias_cap(l)
            if l == 1:
                mixing_matrix()
        select(l)
        if l > 0:
            f_sum(FILL[:3])
        to_list()
        shifted(1)
        if l > 0:
            f_prod(x, FILL[3])
            f_sum(FILL[3:])
        shifted(2)
        shifted_far(4)
        if not last:
            c0, c1, c2, ca = MID
            tables(ca, 0, 1)
            if l > 0:
                f_gate()
            tables(ca, 1, 2)
            winners_out(l)
            tables(c0, 0, 1)
            shifted_far(8)
            tables(ca, 2, 8, 2)
            table_scalar(c2)
            tables(c0, 1, 3)
            if l > 0:
                f_silu()
                f_spread(0)
            tables(c0, 3, 8)
            counts(c0)
            if l > 0:
                f_spread(1)
            tables(c1, 0, 8)
            winners_offsets()
            counts(ca)
            steps_out(ca)
            counts(c1)
            differences(ca)
            tables(c2, 0, 7)
            counts(c2)
            for k, ch in enumerate((c0, c1, ca)):
                new_bias(ch, k)
            if l > 0:
                f_y(x, 1)
            new_bias(c2, 3)
            if l > 0:
                f_y(x, 0)
            else:
                x_constants(2)
            gather_uv(l, 0)
            gather_uv(l, 1, two(rank + 1))
            shift_sums(l)
            if l > 0:
                f_spread(2)
                f_spread(3)
            offsets(0)
            offsets(1)
            if l > 0:
                f_y(x, 2)
            offsets(2)
            shift_tokens()
            if l > 0:
                f_y(x, 3)
                for n in range(-1, N):
                    mix(x, n)
            send_uv(l, SENDS[:3], KB)
        else:
            c0, c1 = END
            f_gate()
            winners_offsets()
            gather_uv(l, 0, two(rank + 1))
            gather_uv(l, 0, ((peers[2], peers[2] + 1),), "V")
            f_silu()
            gather_uv(l, 1, ((0, rank), (rank + 1, N)))
            tables(c0, 0, 1)
            send_uv(l, SENDS)
            for u in range(2):
                gather_uv(l, u, ((rank, rank + 1),))
            for n in range(N):
                f_spread(n, FB)
            mix(x, -1)
            tables(c0, 1, 2)
            for n in (0, 2):
                f_y(x, n, FB, True)
                f_y(x, n + 1, FB)
                tables(c0, n // 2 + 2, n // 2 + 3)
                y_pair(n)
                mix(x, n + 1)
            f_tanh(x, (0,))
            tables(c0, 4, 8)
            last_d(0)
            counts(c0)
            tables(c1, 0, 4)
            last_d(1)
            last_d(2)
            last_silu(0)
            tables(c1, 4, 5)
            last_y(0)
            last_d(3)
            add_x()
            last_mix(0)
            tables(c1, 5, 8)
            last_silu(1)
            counts(c1)
            last_bias(c0)
            for n in range(1, N):
                last_y(n)
                last_mix(n)
                if n < N - 1:
                    last_silu(n + 1)
                if n == 2:
                    last_bias(c1)
            f_tanh(l)
    for s in total:
        if max(seen[q].get(s, 0) for q in Q) < total[s]:
            need("G", (s, total[s]))
